import numpy as np, ml_dtypes
CORES = [16,18,20,22]
N = 4
import mx_ref
BF = ml_dtypes.bfloat16
def gcols(t, e):
    v = np.concatenate([t.reshape(8, 16, -1, 4), np.zeros((8, 16, 1, 4), BF)], axis=2)
    return np.ascontiguousarray(np.stack([v[g][:, e[g]] for g in range(8)])).reshape(128, -1)
def tile(rs):
    return np.stack(rs, axis=2).reshape(128, -1).astype(BF)
def pick(q, e):
    c = np.concatenate([q[0].reshape(128, -1, 4), np.zeros((128, 1, 4), np.uint8)], axis=1); s = np.concatenate([q[1], np.ones((16, 1), np.uint8)], axis=1)
    return (np.ascontiguousarray(c[:, e].reshape(128, -1)), np.ascontiguousarray(s[:, e]))
def join(*qs):
    return (np.concatenate([q[0] for q in qs], axis=1), np.concatenate([q[1] for q in qs], axis=1))
def put(q, e, v):
    c, s = q[0].reshape(128, -1, 4).copy(), q[1].copy(); c[:, e] = v[0].reshape(128, -1, 4); s[:, e] = v[1]
    return (c.reshape(128, -1), s)
def pk(c, s):
    return (np.ascontiguousarray(c), mx_ref.live(s))
def emit(q):
    return q[0], q[1]
def packed(v, rng):
    q = [mx_ref.quantize(np.ascontiguousarray(v[r])) for r in range(N)]
    return np.stack([a for a, b in q]), np.stack([mx_ref.plane(b, rng) for a, b in q])
def values_of_codes():
    e, c = np.zeros((128, 128, 4), np.float32), np.zeros((128, 2, 4), np.uint8)
    e[np.arange(128), np.arange(128), 0] = 1
    c[:127, :, 0] = np.arange(256).reshape(2, 128).T[:127]
    return mx_ref.matmul(mx_ref.quantize(e.reshape(128, 512).astype(BF)), (c.reshape(128, 8), np.full((16, 2), 127, np.uint8))).T.reshape(-1).astype(np.float64)
CODE_VALUE, SCALE_VALUE = values_of_codes(), 2.0 ** (np.arange(256) - 127.0)
def decode(q):
    return (CODE_VALUE[q[0]].reshape(16, 8, -1, 4) * SCALE_VALUE[q[1]][:, None, :, None] + 0.0).reshape(128, -1).astype(np.float32)
def f(rng, *shape):
    return mx_ref.flush((rng.standard_normal(shape, dtype=np.float32) * np.exp2(rng.integers(-2, 3, shape[:-1] + (1,)))).astype(BF))
def wide(rng, *shape, cols=0):
    v = rng.standard_normal(shape, dtype=np.float32) * np.exp2(rng.integers(-12, 13, shape)).astype(np.float32)
    if cols: v *= np.repeat(np.exp2(rng.integers(-cols, cols + 1, shape[:-2] + (1, shape[-1] // 4))) * (rng.random(shape[:-2] + (1, shape[-1] // 4)) > 0.0625), 4, axis=-1).astype(np.float32)
    return mx_ref.flush(v.astype(BF))
C, STEP = 384, [1, 2, 3]
def numbers_of(rng):
    return {"x": np.array(f(rng, N, 128, 4 * C)), "u": np.array(f(rng, N, 128, 512)), "v": np.array(f(rng, N, 128, 512))}
def layers(rng):
    return np.array(f(rng, N, 128, 2048)).reshape(N, 8, 16, 4, 8, 16, 4)
def weights(rng, w):
    c, p = packed(np.ascontiguousarray(w).reshape(N, 128, 2048), rng)
    return {"wc": c, "ws": p}
def both(x, u):
    return {"x": x.astype(np.float32).reshape(N, 128, 4 * C).astype(BF), "u": u.astype(np.float32).reshape(N, 128, 512).astype(BF)}
def setup_inputs(rng):
    return {**numbers_of(rng), **weights(rng, layers(rng))}
def setup_inputs_ties(rng):
    d = numbers_of(rng)
    e = rng.permutation(N)
    x = rng.integers(-1, 2, (N, 128, C, 4)) * (rng.random((N, 128, C, 4)) < 0.09375)
    u = rng.integers(-1, 2, (N, 128, 128, 4)) * (rng.random((N, 128, 128, 4)) < 0.09375)
    x[e[0]] = x[e[0]][:, :1].copy()
    x[e[1]] = 0
    u[e[2]] = u[e[2]][:, :1].copy()
    w = np.zeros((N, 128, 512, 4), np.float32)
    for r in range(N):
        a, c = rng.permutation(512)[:128], rng.permutation(512)[:128]
        w[r, a // 4, c, a % 4] = 64
    return {**both(x, u), "v": d["v"], **weights(rng, w.astype(BF))}
def setup_inputs_near(rng):
    d = numbers_of(rng)
    h, o = rng.permutation(8), rng.permutation(N) % 4
    x = d["x"].astype(np.float32).reshape(N, 8, 16, C, 4)
    u = d["u"].astype(np.float32).reshape(N, 8, 16, 128, 4)
    x[:, :, 8:] = 0
    u[:, :, :8] = 0
    x[:, h[:2], :8] = 0
    p = np.exp2(np.arange(4) - 23.0)
    for r in range(N):
        k = 1.0 if o[r] < 2 else 2.0 ** -29
        if o[r] == 3:
            x[r, h[0], 0, :, 0] = rng.choice([1.0, 1.125], C) * 2.0 ** -30
            u[r, h[0], 0, :, 0] = rng.choice([1.125, 1.25], 128) * 2.0 ** -30
        else:
            x[r, h[0], 0, :, 0] = -1.0 if o[r] == 1 else 1.0
            u[r, h[0], 0, :, 0] = k
            x[r, h[1], 0] = ((rng.integers(0, 16, (C, 1)) >> np.arange(4)) & 1) * p
            u[r, h[1], 0] = k
            x[r, h[1], 1] = p
            u[r, h[1], 1] = ((rng.integers(0, 16, (128, 1)) >> np.arange(4)) & 1) * k
            x[r, h[1], 2, :, 0] = 2.0 ** -10
            u[r, h[1], 2, :, 0] = k
        x[r, h[0], 0, rng.integers(C), 0] = 2.0 ** 29
    w = layers(rng)
    w[:, h[:2], :8] = 0
    for g in h[:2]: w[:, :, :, :, g, :8] = 0
    return {**both(x, u), "v": d["v"], **weights(rng, w)}
def setup_inputs_huge(rng):
    d = numbers_of(rng)
    e = rng.permutation(N)
    x = 0.7 + 0.3 * rng.random((N, 8, 16, C, 4))
    u = 0.7 + 0.3 * rng.random((N, 8, 16, 128, 4))
    for i in range(N):
        r = e[i]
        if i == 0:
            x[r] = -0.94 - 0.06 * rng.random((8, 16, C, 4))
            x[r][:, :, rng.permutation(C)[:4]] *= -1.0
            u[r] = 0.94 + 0.06 * rng.random((8, 16, 128, 4))
        elif i % 2 == 1: u[r] *= -1.0
        else:
            x[r] *= rng.choice([-1.0, 1.0], (1, 1, C, 1))
            u[r] *= rng.choice([-1.0, 1.0], (1, 1, 128, 1))
    w = np.zeros((N, 128, 4, 128, 4), np.float32)
    i = np.arange(128)
    for b in range(4): w[:, i, b, i, b] = -1
    return {**both(x * 2.0 ** 30, u * 2.0 ** 30), "v": d["v"], **weights(rng, w.astype(BF))}
def setup_inputs_odd(rng):
    d = numbers_of(rng)
    x = d["x"].astype(np.float32).reshape(N, 8, 16, C, 4)
    u = d["u"].astype(np.float32).reshape(N, 8, 16, 128, 4)
    for a, n in ((x, C), (u, 128)):
        a[:, :, :8] = (2 * rng.integers(0, 8, (N, 8, 8, n, 4)) + 1) * rng.choice([-1.0, 1.0], (N, 8, 8, n, 4)) * 2.0 ** -16
        a[:, :, 0, :, 0] = rng.choice([1.625, 1.75, 1.875, 1.96875], (N, 8, n))
        a[:, :, 8] = 0
        a[:, :, 8, :, 0] = 1
    w = layers(rng)
    w[:, :, :, :, :, :9] = 0
    for g in range(8): w[:, g, 8, 0, g, 0, 0] = 3
    return {**both(x, u), "v": d["v"], **weights(rng, w)}
def setup_inputs_spread(rng):
    d = setup_inputs(rng)
    d["x"] = wide(rng, N, 128, 4 * C, cols=6)
    return d
def check_inputs(d):
    b = []
    for k in ("x", "u", "v"):
        a = np.abs(d[k].astype(np.float32))
        if not (np.isfinite(a).all() and ((a == 0) | (a >= 2.0 ** -30) & (a <= 2.0 ** 30)).all()): b.append("a value of " + k)
    none, least, most = [emit(mx_ref.quantize(np.full((128, 16), k, np.float32).astype(BF)))[1][0, 0] for k in (0.0, 2.0 ** -30, 2.0 ** 30)]
    for r in range(N):
        if ((d["wc"][r] == 0x7F) | (d["wc"][r] == 0xFF)).any(): b.append("wc: a code that is no number")
        s = mx_ref.live(d["ws"][r])
        if ((s != none) & ((s < least) | (s > most))).any(): b.append("ws: a scale out of range")
    return b
def reference(x, u, v, wc, ws):
    lay = [pk(wc[r], ws[r]) for r in range(N)]
    now = [mx_ref.quantize(x[r]) for r in range(N)]
    stat = [mx_ref.quantize(u[r]) for r in range(N)]
    down, along = np.zeros((N, 8, C), np.int64), np.zeros((N, 8, 128), np.int64)
    for h in STEP:
        sent = []
        for r in range(N):
            own = decode(now[r])
            s = mx_ref.matmul(stat[r], now[r]) + np.float32(0.0)
            down[r] = np.argmax(s.reshape(8, 16, C), axis=1) + 16 * np.arange(8)[:, None]
            along[r] = np.argsort(-s, axis=1, kind="stable")[:, :8].T
            a = gcols(decode(stat[r]).astype(BF), down[r]).astype(np.float32)
            z = mx_ref.quantize(((own + a) * np.float32(0.5)).astype(BF))
            now[r] = mx_ref.quantize(tile([mx_ref.matmul(pick(lay[r], np.arange(128 * b, 128 * b + 128)), z) * np.float32(0.03125) + own[:, b::4] for b in range(4)]))
            sent.append(mx_ref.quantize(gcols(decode(now[r]).astype(BF), along[r])))
        stat = [sent[(r - h) % N] for r in range(N)]
    y, op = np.zeros((N, 128, C), np.float32), np.zeros((N, 8, C + 128), np.float32)
    oc, osc = np.zeros((N, 128, 4 * C), np.uint8), np.zeros((N, 16, C), np.uint8)
    uc, usc = np.zeros((N, 128, 512), np.uint8), np.zeros((N, 16, 128), np.uint8)
    for r in range(N):
        y[r] = mx_ref.matmul(mx_ref.quantize(v[r]), now[r])
        op[r, :, :C] = down[r]
        op[r, :, C:] = along[r]
        oc[r], osc[r] = emit(now[r])
        uc[r], usc[r] = emit(stat[r])
    return {"y": y, "op": op, "oc": oc, "osc": osc, "uc": uc, "usc": usc}

@@ -1,0 +1,292 @@
+from concourse.bass import DstId, RemoteDMATransfer
+from concourse.mybir import dt, AluOpType as A, AxisListType, ActivationFunctionType as F
+
+N, C, U, STEP = 4, 384, 128, (1, 2, 3)
+BIG = 1e29
+HW = 388
+GW = 2 * 16
+
+
+def _sb(n, d):
+    return ("sbuf", [128, n], d)
+
+
+CODE, PL, BF, F32, U16, I32 = "float8_e4m3fn_x4", "uint8", "bfloat16", "float32", "uint16", "int32"
+SCRATCH = {
+    "xin": _sb(4 * C, BF), "uin": _sb(512, BF), "vin": _sb(512, BF),
+    "wq": _sb(512, CODE), "wz": _sb(512, PL), "vq": _sb(128, CODE), "vz": _sb(128, PL),
+    "c32": _sb(128, BF), "eye": _sb(128, BF), "pidx": _sb(1, I32), "pi2": _sb(2, I32), "pf": _sb(4, F32),
+    "ef": _sb(2048, BF), "ee": _sb(2048, BF), "eo": _sb(2048, BF),
+    "efq": _sb(512, CODE), "efz": _sb(512, PL), "eeq": _sb(512, CODE), "eez": _sb(512, PL),
+    "eoq": _sb(512, CODE), "eoz": _sb(512, PL),
+    "cap": _sb(C, F32), "ones": _sb(8, F32),
+    "st": _sb(C, F32), "ex": _sb(C, F32), "nr": _sb(C, BF), "tr": _sb(C, BF),
+    "k32": _sb(32, F32), "kt": ("sbuf", [128, 2, 16], F32), "kd": ("sbuf", [128, 2, 2, 16], F32), "ko": ("sbuf", [128, 2, 32], F32),
+    "n32": _sb(32, F32), "nt": ("sbuf", [128, 2, 16], F32), "nd": ("sbuf", [128, 2, 2, 16], F32), "no": ("sbuf", [128, 2, 32], F32),
+    "xn": ("sbuf", [128, 4, 2, 2], F32), "cn": _sb(8, F32),
+    "hist": _sb(9 * HW, F32), "ep": _sb(8, F32), "ob": _sb(8, F32), "junk": _sb(C, BF),
+    "zt": _sb(4 * C, BF), "xt": _sb(4 * C, BF), "vt": _sb(512, BF), "yt": _sb(C, F32),
+    "xq0": _sb(C, CODE), "xz0": _sb(C, PL), "uq0": _sb(128, CODE), "uz0": _sb(128, PL),
+}
+for _g in range(1, 8):
+    SCRATCH["f%d" % _g] = _sb(C, BF)
+    SCRATCH["q%d" % _g] = _sb(C, BF)
+for _h in (1, 2, 3):
+    SCRATCH.update({
+        "xq%d" % _h: _sb(C, CODE), "xz%d" % _h: _sb(C, PL), "uq%d" % _h: _sb(128, CODE), "uz%d" % _h: _sb(128, PL),
+        "zq%d" % _h: _sb(C, CODE), "zz%d" % _h: _sb(C, PL),
+        "aeq%d" % _h: _sb(C, CODE), "aez%d" % _h: _sb(C, PL), "aoq%d" % _h: _sb(C, CODE), "aoz%d" % _h: _sb(C, PL),
+        "veq%d" % _h: _sb(128, CODE), "vez%d" % _h: _sb(128, PL), "voq%d" % _h: _sb(128, CODE), "voz%d" % _h: _sb(128, PL),
+        "sq%d" % _h: _sb(128, CODE), "sz%d" % _h: _sb(128, PL),
+        "ok%d" % _h: _sb(48, U16), "on%d" % _h: _sb(16, U16)})
+for _b in range(8):
+    SCRATCH["p%d" % _b] = ("psum", [128, 512], F32)
+
+SEMAPHORES = ["cv", "cs", "ct", "cp", "sent", "rc1", "rc2", "rc3", "outy", "outs"] + ["d%d" % i for i in range(12)]
+
+
+def rank_program(g, core, T, topo):
+    rank = T.rank_of(core)
+    if rank is None:
+        return
+    queues = {"v": g.vector, "s": g.scalar, "t": g.tensor, "p": g, "y": g.sync}
+    count, seen, lastw, readers, nd = {}, {q: {} for q in queues}, {}, {}, [0]
+
+    def wait(qn, tok):
+        sem, val = tok
+        if seen[qn].get(sem, 0) < val:
+            queues[qn].wait_ge(T.sem[sem], val)
+            seen[qn][sem] = val
+
+    def before(qn, r, w):
+        need = {}
+        own = "c" + qn
+        for k in r:
+            for s, v in lastw.get(k, {}).items():
+                need[s] = max(need.get(s, 0), v)
+        for k in w:
+            for s, v in lastw.get(k, {}).items():
+                if not (qn == "t" and s == own):
+                    need[s] = max(need.get(s, 0), v)
+            for s, v in readers.get(k, {}).items():
+                if s != own:
+                    need[s] = max(need.get(s, 0), v)
+        for s in sorted(need):
+            wait(qn, (s, need[s]))
+
+    def after(tok, r, w):
+        for k in w:
+            lastw[k] = {tok[0]: tok[1]}
+            readers[k] = {}
+        for k in r:
+            readers.setdefault(k, {})[tok[0]] = tok[1]
+
+    def op(qn, f, r, w):
+        before(qn, r, w)
+        sem = "c" + qn
+        count[sem] = count.get(sem, 0) + 1
+        f().then_inc(T.sem[sem], 1)
+        after((sem, count[sem]), r, w)
+
+    def dma(qn, out, in_, r, w, sem=None):
+        before(qn, r, w)
+        if sem is None:
+            sem = "d%d" % nd[0]
+            nd[0] += 1
+        count[sem] = count.get(sem, 0) + 16
+        queues[qn].dma_start(out, in_).then_inc(T.sem[sem], 16)
+        after((sem, count[sem]), r, w)
+
+    v, s, t = g.vector, g.scalar, g.tensor
+    P = [T["p%d" % b] for b in range(8)]
+
+    def mm(bank, n, lq, lz, a, rq, rz, start, stop, extra=()):
+        op("t", lambda: t.matmul_mx(P[bank][:, 0:n], T[lq][:, a:a + 128], T[lz][:, a:a + 128], T[rq][:], T[rz][:], start, stop),
+           [lq, lz, rq, rz], ["p%d" % bank])
+
+    def quant(q, z, tile, a=None, b=None, key=None):
+        if a is None:
+            op("v", lambda: v.quantize_mx(T[q][:], T[z][:], T[tile][:]), [tile], [q, z])
+        else:
+            op("v", lambda: v.quantize_mx(T[q][:, a:b], T[z][:, a:b], T[tile][:, 4 * a:4 * b]), [key], [q, z])
+
+    def cp(qn, out, in_, r, w, scale=None):
+        if qn == "v":
+            if scale is None:
+                op("v", lambda: v.tensor_copy(out, in_), r, w)
+            else:
+                op("v", lambda: v.tensor_scalar(out, in_, scale, None, A.mult), r, w)
+        else:
+            op("s", lambda: s.activation(out, in_, F.Copy, scale=1.0 if scale is None else scale), r, w)
+
+    def pick(dq, dz, sq, sz, off, a, b):
+        op("v", lambda: v.tensor_copy(T[dq][:].bitcast(dt.uint32), T[sq][:].bitcast(dt.uint32).indirect(T[off][:, a:b])), [sq, off], [dq])
+        op("s", lambda: s.activation(T[dz][:], T[sz][:].indirect(T[off][:, a:b]), F.Copy), [sz, off], [dz])
+
+    dma("y", T.uin[:], T.u[:], [], ["uin"])
+    dma("s", T.xin[:, 0:512], T.x[:, 0:512], [], ["xin0"])
+    dma("y", T.xin[:, 512:1024], T.x[:, 512:1024], [], ["xin1"])
+    dma("s", T.xin[:, 1024:1536], T.x[:, 1024:1536], [], ["xin2"])
+    dma("y", T.wq[:].bitcast(dt.uint8), T.wc[:], [], ["wq"])
+    dma("y", T.wz[:], T.ws[:], [], ["wz"])
+    dma("y", T.vin[:], T.v[:], [], ["vin"])
+
+    op("p", lambda: g.iota(T.pidx[:], [[0, 1]], 0, 1), [], ["pidx"])
+    op("v", lambda: v.memset(T.c32[:], 32.0), [], ["c32"])
+    op("p", lambda: g.affine_select(T.eye[:], T.c32[:], [[-1, 128]], A.is_equal, 0.0, 0, 1), ["c32"], ["eye"])
+    op("v", lambda: v.memset(T.ef[:], 0.0), [], ["ef"])
+    op("v", lambda: v.tensor_scalar(T.pi2[:, 0:1], T.pidx[:], 16, None, A.bitwise_and), ["pidx"], ["pi2a"])
+    op("v", lambda: v.tensor_scalar(T.pi2[:, 1:2], T.pidx[:], 5, None, A.arith_shift_right), ["pidx"], ["pi2b"])
+    op("v", lambda: v.tensor_scalar(T.pf[:, 0:1], T.pi2[:, 0:1], -0.0625, 1.0, A.mult, A.add), ["pi2a"], ["even"])
+    op("v", lambda: v.tensor_scalar(T.pf[:, 1:2], T.pi2[:, 0:1], 0.0625, None, A.mult), ["pi2a"], ["odd"])
+    op("v", lambda: v.tensor_scalar(T.pf[:, 2:3], T.pi2[:, 1:2], 32.0, 15.0, A.mult, A.add), ["pi2b"], ["base0"])
+    op("v", lambda: v.tensor_scalar(T.pf[:, 3:4], T.pi2[:, 1:2], 32.0, 31.0, A.mult, A.add), ["pi2b"], ["base1"])
+    for b in range(4):
+        cp("v", T.ef[:, 512 * b + b:512 * (b + 1):4], T.eye[:], ["eye", "ef"], ["efb%d" % b])
+    efk = ["ef"] + ["efb%d" % b for b in range(4)]
+    op("s", lambda: s.activation(T.eo[:], T.ef[:], F.Copy, scale=T.pf[:, 1:2]), efk + ["odd"], ["eo"])
+    op("v", lambda: v.quantize_mx(T.efq[:], T.efz[:], T.ef[:]), efk, ["efq", "efz"])
+    op("v", lambda: v.tensor_scalar(T.ee[:], T.ef[:], T.pf[:, 0:1], None, A.mult), efk + ["even"], ["ee"])
+    op("v", lambda: v.quantize_mx(T.eeq[:], T.eez[:], T.ee[:]), ["ee"], ["eeq", "eez"])
+    op("v", lambda: v.memset(T.cap[:], BIG), [], ["cap"])
+    op("v", lambda: v.memset(T.cap[:, 0:C:16], -BIG), [], ["cap"])
+    op("v", lambda: v.memset(T.ex[:, 0:1], -BIG), [], ["ex"])
+    op("v", lambda: v.memset(T.k32[:], 0.0), [], ["k32"])
+    quant("uq0", "uz0", "uin")
+    for i in range(3):
+        quant("xq0", "xz0", "xin", 128 * i, 128 * i + 128, "xin%d" % i)
+    op("v", lambda: v.quantize_mx(T.eoq[:], T.eoz[:], T.eo[:]), ["eo"], ["eoq", "eoz"])
+    op("v", lambda: v.memset(T.n32[:], 0.0), [], ["n32"])
+    op("v", lambda: v.memset(T.ones[:], 1.0), [], ["ones"])
+    op("v", lambda: v.memset(T.ep[:], 0.0), [], ["ep"])
+    op("v", lambda: v.memset(T.hist[:, 0:HW], BIG), [], ["h0"])
+    op("v", lambda: v.memset(T.hist[:, HW:9 * HW:HW], -BIG), [], ["h%d" % k for k in range(1, 9)])
+
+    ZB, RB, SB = (1, 2, 3, 4), (5, 6, 7, 1), 0
+
+    def hv(k):
+        return T.hist[:, HW * k + C:HW * k + C + 1]
+
+    def top8(rd):
+        S = P[SB][:, 0:C]
+        for k in range(1, 9):
+            op("v", lambda: v.tensor_tensor_scan(T.hist[:, HW * k + 1:HW * k + 1 + C], S, T.hist[:, HW * (k - 1):HW * (k - 1) + C], -BIG, A.max, A.min),
+               ["p0", "h%d" % (k - 1)], ["h%d" % k])
+            if k == 1:
+                yield
+            else:
+                yield
+        op("v", lambda: v.tensor_tensor(T.ep[:, 1:8], T.hist[:, 2 * HW + C:9 * HW:HW], T.hist[:, HW + C:8 * HW:HW], A.is_equal),
+           ["h%d" % k for k in range(1, 9)], ["ep"])
+        op("s", lambda: s.activation(T.junk[:], T.hist[:, HW + 1:HW + 1 + C], F.Sign, bias=hv(1), scale=-1.0, accum_out=T.n32[:, 0:1]),
+           ["h1"], ["junk", "n32a"])
+        yield
+        for gg in range(1, 8):
+            op("v", lambda: v.tensor_scalar(T["f%d" % gg][:], S, hv(gg + 1), None, A.is_equal), ["p0", "h%d" % (gg + 1)], ["f%d" % gg])
+            if gg == 1:
+                op("v", lambda: v.tensor_tensor_scan(T.ob[:], T.ep[:], T.ones[:], 0.0, A.mult, A.add), ["ep", "ones"], ["ob"])
+            yield
+            op("v", lambda: v.tensor_tensor_scan(T["q%d" % gg][:], T["f%d" % gg][:], T["f%d" % gg][:], 0.5, A.add, A.max), ["f%d" % gg], ["q%d" % gg])
+            op("s", lambda: s.activation(T.junk[:], T["q%d" % gg][:], F.Sign, bias=T.ob[:, gg:gg + 1], scale=-1.0, accum_out=T.cn[:, gg:gg + 1]),
+               ["q%d" % gg, "ob"], ["junk", "cn"])
+            yield
+
+    def spread(src, tb, db, ob):
+        op("v", lambda: v.transpose(T[tb][:], T[src][:]), [src] if src == "k32" else [src, "n32a"], [tb])
+        for i in range(2):
+            cp("v", T[db][:, :, i, :], T[tb][:], [tb], [db + str(i)])
+        op("v", lambda: v.transpose(T[ob][:], T[db][:]), [db + "0", db + "1"], [ob])
+
+    for rd in (1, 2, 3):
+        xq, xz, uq, uz = "xq%d" % (rd - 1), "xz%d" % (rd - 1), "uq%d" % (rd - 1), "uz%d" % (rd - 1)
+        nq, nz = "xq%d" % rd, "xz%d" % rd
+        if rd > 1:
+            for b in range(4):
+                mm(ZB[b], C, "efq", "efz", 128 * b, xq, xz, True, False)
+        mm(SB, C, uq, uz, 0, xq, xz, True, True)
+        if rd == 1:
+            for b in range(4):
+                mm(ZB[b], C, "efq", "efz", 128 * b, xq, xz, True, False)
+        for b in range(3):
+            mm(RB[b], C, "efq", "efz", 128 * b, xq, xz, True, False)
+        op("v", lambda: v.transpose(T.st[:], P[SB][:, 0:C]), ["p0"], ["st"])
+        op("v", lambda: v.tensor_tensor_scan(T.ex[:, 1:C], T.st[:, 0:C - 1], T.cap[:, 1:C], -BIG, A.max, A.min), ["st", "cap"], ["ex"])
+        op("v", lambda: v.tensor_tensor(T.nr[:], T.st[:], T.ex[:], A.is_le), ["st", "ex"], ["nr"])
+        op("v", lambda: v.tensor_tensor_scan(T.tr[:], T.nr[:], T.nr[:], 0.0, A.mult, A.add), ["nr"], ["tr"])
+        for i in range(2):
+            op("v", lambda: v.tensor_scalar(T.k32[:, 12 * i:12 * i + 12], T.tr[:, 15 + 16 * i:C:32], -1.0, T.pf[:, 2 + i:3 + i], A.mult, A.add),
+               ["tr", "base%d" % i], ["k32"])
+        spread("k32", "kt", "kd", "ko")
+        ok = "ok%d" % rd
+        for i in range(2):
+            for hh in range(2):
+                cp("v", T[ok][:, 24 * i + hh:24 * i + 24:2], T.ko[:, hh, 12 * i:12 * i + 12], ["ko"], [ok])
+        pick("aeq%d" % rd, "aez%d" % rd, uq, uz, ok, 0, 24)
+        pick("aoq%d" % rd, "aoz%d" % rd, uq, uz, ok, 24, 48)
+        for b in range(4):
+            mm(ZB[b], C, "eeq", "eez", 128 * b, "aeq%d" % rd, "aez%d" % rd, False, False)
+        for b in range(4):
+            mm(ZB[b], C, "eoq", "eoz", 128 * b, "aoq%d" % rd, "aoz%d" % rd, False, True)
+        for b in range(4):
+            cp("s", T.zt[:, b:4 * C:4], P[ZB[b]][:, 0:C], ["p%d" % ZB[b]], ["zt%d" % b], 1.0 / 64)
+        fill = top8(rd)
+        for i in range(7):
+            next(fill, None)
+        mm(RB[3], C, "efq", "efz", 384, xq, xz, True, False)
+        op("v", lambda: v.quantize_mx(T["zq%d" % rd][:], T["zz%d" % rd][:], T.zt[:]), ["zt%d" % b for b in range(4)], ["zq%d" % rd, "zz%d" % rd])
+        for b in range(4):
+            mm(RB[b], C, "wq", "wz", 128 * b, "zq%d" % rd, "zz%d" % rd, False, True)
+        for b in range(4):
+            cp("s", T.xt[:, b:4 * C:4], P[RB[b]][:, 0:C], ["p%d" % RB[b]], ["xt%d" % b], 1.0 / 32)
+        for i in range(9):
+            next(fill, None)
+        op("v", lambda: v.quantize_mx(T[nq][:], T[nz][:], T.xt[:]), ["xt%d" % b for b in range(4)], [nq, nz])
+        for _ in fill:
+            pass
+        if rd == 3:
+            quant("vq", "vz", "vin")
+            mm(5, C, "vq", "vz", 0, nq, nz, True, True)
+        op("v", lambda: v.tensor_scalar(T.n32[:, 1:8], T.cn[:, 1:8], 0.5, 192.0, A.mult, A.add), ["cn"], ["n32"])
+        spread("n32", "nt", "nd", "no")
+        for a in range(4):
+            for G in range(4):
+                cp("v" if (a + G) % 2 else "s", T.xn[32 * G:32 * G + 32, a, :, :], T.no[32 * a:32 * a + 32, :, 2 * G:2 * G + 2], ["no"], ["xn%d%d" % (a, G)])
+        on = "on%d" % rd
+        for i in range(2):
+            cp("v", T[on][:, 8 * i:8 * i + 8], T.xn[:, :, :, i], ["xn%d%d" % (a, G) for a in range(4) for G in range(4)], [on])
+        pick("veq%d" % rd, "vez%d" % rd, nq, nz, on, 0, 8)
+        pick("voq%d" % rd, "voz%d" % rd, nq, nz, on, 8, 16)
+        for b in range(4):
+            mm(ZB[b], 128, "eeq", "eez", 128 * b, "veq%d" % rd, "vez%d" % rd, True, False)
+        for b in range(4):
+            mm(ZB[b], 128, "eoq", "eoz", 128 * b, "voq%d" % rd, "voz%d" % rd, False, True)
+        for b in range(4):
+            cp("vs"[b % 2], T.vt[:, b:512:4], P[ZB[b]][:, 0:128], ["p%d" % ZB[b]], ["vt%d" % b], 1.0 / 32)
+        op("v", lambda: v.quantize_mx(T["sq%d" % rd][:], T["sz%d" % rd][:], T.vt[:]), ["vt%d" % b for b in range(4)], ["sq%d" % rd, "sz%d" % rd])
+        dst = T.cores[(rank + STEP[rd - 1]) % N]
+        rid, pid, _ = topo.addr(dst)
+        eng = topo.engines(core, dst)
+        half = len(eng) // 2
+        m1 = sum(1 << e for e in eng[:half])
+        m2 = sum(1 << e for e in eng[half:])
+        before("p", ["sq%d" % rd, "sz%d" % rd], [])
+        g.remote_dma(T["uq%d" % rd][:].bitcast(dt.uint8), T["sq%d" % rd][:].bitcast(dt.uint8), T.sem["rc%d" % rd], T.sem["sent"], pid, rid, m1)
+        g.remote_dma(T["uz%d" % rd][:], T["sz%d" % rd][:], T.sem["rc%d" % rd], T.sem["sent"], pid, rid, m2)
+        count["sent"] = count.get("sent", 0) + len(eng)
+        count["rc%d" % rd] = len(eng)
+        for k in ("uq%d" % rd, "uz%d" % rd):
+            lastw[k] = {"rc%d" % rd: len(eng)}
+
+    cp("s", T.yt[:], P[5][:, 0:C], ["p5"], ["yt"])
+    dma("y", T.oc[:], T.xq3[:].bitcast(dt.uint8), ["xq3"], [], "outy")
+    for k in range(4):
+        dma("y", T.osc[4 * k:4 * k + 4, :], T.xz3[32 * k:32 * k + 4, :], ["xz3"], [], "outy")
+    for a in range(4):
+        dma("y", T.op[2 * a:2 * a + 2, 0:C], T.kt[32 * a:32 * a + 24, :, :], ["kt"], [], "outy")
+        dma("y", T.op[0:8, C + 32 * a:C + 32 * a + 32], T.nt[32 * a:32 * a + 8, :, :], ["nt"], [], "outy")
+    dma("s", T.y[:], T.yt[:], ["yt"], [], "outs")
+    dma("s", T.uc[:], T.uq3[:].bitcast(dt.uint8), ["uq3"], [], "outs")
+    for k in range(4):
+        dma("y" if k % 2 else "s", T.usc[4 * k:4 * k + 4, :], T.uz3[32 * k:32 * k + 4, :], ["uz3"], [], "outy" if k % 2 else "outs")
+    for sem in sorted(count):
+        wait("p", (sem, count[sem]))

@@ -1,10 +1,11 @@
-from concourse.bass import DstId, RemoteDMATransfer
-from concourse.mybir import dt, AluOpType as A, AxisListType, ActivationFunctionType as F
+from concourse.mybir import dt, AluOpType as A, ActivationFunctionType as F
 
 N, C, U, STEP = 4, 384, 128, (1, 2, 3)
 BIG = 1e29
 HW = 388
-GW = 2 * 16
+PAR = {"down": (0, 1, 1, 1, 1, 0, 1, 0, 1), "z": (5, 4), "x": (12, 0), "zv": (), "xv": (2, 3), "dma": (0, 1), "vm": (), "ea": (3, 5), "eb": (1, 2),
+       "seq": "M1 M2 E1 M3 M4 M5 E2 E3 O1 H2 H1 B1 H3 M6 E5 Q3 E4 M7 H4 Q2 M8 O2 Q1 H5 B2 Q4 Q5 E7 E6 H6 H7 Q7 Q6"}
+HALF = ((0, 192), (192, 384))
 
 
 def _sb(n, d):
@@ -15,34 +16,31 @@ CODE, PL, BF, F32, U16, I32 = "float8_e4m3fn_x4", "uint8", "bfloat16", "float32"
 SCRATCH = {
     "xin": _sb(4 * C, BF), "uin": _sb(512, BF), "vin": _sb(512, BF),
     "wq": _sb(512, CODE), "wz": _sb(512, PL), "vq": _sb(128, CODE), "vz": _sb(128, PL),
-    "c32": _sb(128, BF), "eye": _sb(128, BF), "pidx": _sb(1, I32), "pi2": _sb(2, I32), "pf": _sb(4, F32),
+    "c32": _sb(512, BF), "codd": _sb(512, BF), "eye": _sb(128, BF), "pidx": _sb(1, I32), "pi2": _sb(6, I32), "pf": _sb(8, F32),
     "ef": _sb(2048, BF), "ee": _sb(2048, BF), "eo": _sb(2048, BF),
     "efq": _sb(512, CODE), "efz": _sb(512, PL), "eeq": _sb(512, CODE), "eez": _sb(512, PL),
     "eoq": _sb(512, CODE), "eoz": _sb(512, PL),
-    "cap": _sb(C, F32), "ones": _sb(8, F32),
+    "cap": _sb(C, F32), "ones": _sb(8, F32), "one": _sb(C, BF), "ssb": _sb(C, F32),
     "st": _sb(C, F32), "ex": _sb(C, F32), "nr": _sb(C, BF), "tr": _sb(C, BF),
-    "k32": _sb(32, F32), "kt": ("sbuf", [128, 2, 16], F32), "kd": ("sbuf", [128, 2, 2, 16], F32), "ko": ("sbuf", [128, 2, 32], F32),
-    "n32": _sb(32, F32), "nt": ("sbuf", [128, 2, 16], F32), "nd": ("sbuf", [128, 2, 2, 16], F32), "no": ("sbuf", [128, 2, 32], F32),
-    "xn": ("sbuf", [128, 4, 2, 2], F32), "cn": _sb(8, F32),
-    "hist": _sb(9 * HW, F32), "ep": _sb(8, F32), "ob": _sb(8, F32), "junk": _sb(C, BF),
+    "k32": _sb(32, F32), "kt": ("sbuf", [128, 2, 16], F32), "kd": ("sbuf", [128, 2, 2, 16], F32), "ko": _sb(64, F32),
+    "n32": _sb(32, F32), "nt": ("sbuf", [128, 2, 16], F32), "nd": ("sbuf", [128, 2, 2, 16], F32), "no": _sb(64, F32),
+    "nop": ("sbuf", [128, 2, 16], F32), "cn": _sb(8, F32), "n0": _sb(1, F32), "it8": _sb(4, F32), "ordk": _sb(4, U16), "ordn": _sb(2, U16),
+    "hist": _sb(9 * HW, F32), "ep": _sb(8, F32), "ob": _sb(8, F32), "sg": _sb(8 * C, BF), "fl": _sb(8 * C, BF), "cu": _sb(8 * C, BF),
+    "junk0": _sb(C, BF), "junk1": _sb(C, BF), "junk2": _sb(C, BF),
     "zt": _sb(4 * C, BF), "xt": _sb(4 * C, BF), "vt": _sb(512, BF), "yt": _sb(C, F32),
     "xq0": _sb(C, CODE), "xz0": _sb(C, PL), "uq0": _sb(128, CODE), "uz0": _sb(128, PL),
-}
-for _g in range(1, 8):
-    SCRATCH["f%d" % _g] = _sb(C, BF)
-    SCRATCH["q%d" % _g] = _sb(C, BF)
+    "zq": _sb(C, CODE), "zz": _sb(C, PL), "ok": _sb(48, U16)}
 for _h in (1, 2, 3):
     SCRATCH.update({
         "xq%d" % _h: _sb(C, CODE), "xz%d" % _h: _sb(C, PL), "uq%d" % _h: _sb(128, CODE), "uz%d" % _h: _sb(128, PL),
-        "zq%d" % _h: _sb(C, CODE), "zz%d" % _h: _sb(C, PL),
         "aeq%d" % _h: _sb(C, CODE), "aez%d" % _h: _sb(C, PL), "aoq%d" % _h: _sb(C, CODE), "aoz%d" % _h: _sb(C, PL),
         "veq%d" % _h: _sb(128, CODE), "vez%d" % _h: _sb(128, PL), "voq%d" % _h: _sb(128, CODE), "voz%d" % _h: _sb(128, PL),
-        "sq%d" % _h: _sb(128, CODE), "sz%d" % _h: _sb(128, PL),
-        "ok%d" % _h: _sb(48, U16), "on%d" % _h: _sb(16, U16)})
+        "sq%d" % _h: _sb(128, CODE), "sz%d" % _h: _sb(128, PL), "on%d" % _h: _sb(16, U16)})
 for _b in range(8):
     SCRATCH["p%d" % _b] = ("psum", [128, 512], F32)
 
-SEMAPHORES = ["cv", "cs", "ct", "cp", "sent", "rc1", "rc2", "rc3", "outy", "outs"] + ["d%d" % i for i in range(12)]
+SEMAPHORES = (["cv", "cs", "ct", "cp", "sent", "rc1", "rc2", "rc3", "outy", "outs"] + ["d%d" % i for i in range(12)]
+              + ["m%d%d" % (h, i) for h in (1, 2, 3) for i in range(4)])
 
 
 def rank_program(g, core, T, topo):
@@ -50,7 +48,7 @@ def rank_program(g, core, T, topo):
     if rank is None:
         return
     queues = {"v": g.vector, "s": g.scalar, "t": g.tensor, "p": g, "y": g.sync}
-    count, seen, lastw, readers, nd = {}, {q: {} for q in queues}, {}, {}, [0]
+    count, seen, lastw, readers, nd, njunk = {}, {q: {} for q in queues}, {}, {}, [0], [0]
 
     def wait(qn, tok):
         sem, val = tok
@@ -100,15 +98,9 @@ def rank_program(g, core, T, topo):
     v, s, t = g.vector, g.scalar, g.tensor
     P = [T["p%d" % b] for b in range(8)]
 
-    def mm(bank, n, lq, lz, a, rq, rz, start, stop, extra=()):
-        op("t", lambda: t.matmul_mx(P[bank][:, 0:n], T[lq][:, a:a + 128], T[lz][:, a:a + 128], T[rq][:], T[rz][:], start, stop),
-           [lq, lz, rq, rz], ["p%d" % bank])
-
-    def quant(q, z, tile, a=None, b=None, key=None):
-        if a is None:
-            op("v", lambda: v.quantize_mx(T[q][:], T[z][:], T[tile][:]), [tile], [q, z])
-        else:
-            op("v", lambda: v.quantize_mx(T[q][:, a:b], T[z][:, a:b], T[tile][:, 4 * a:4 * b]), [key], [q, z])
+    def mm(bank, lq, lz, a, rq, rz, c, d, keys, start, stop):
+        op("t", lambda: t.matmul_mx(P[bank][:, 0:d - c], T[lq][:, a:a + 128], T[lz][:, a:a + 128], T[rq][:, c:d], T[rz][:, c:d], start, stop),
+           [lq] + keys, ["p%d" % bank])
 
     def cp(qn, out, in_, r, w, scale=None):
         if qn == "v":
@@ -119,174 +111,264 @@ def rank_program(g, core, T, topo):
         else:
             op("s", lambda: s.activation(out, in_, F.Copy, scale=1.0 if scale is None else scale), r, w)
 
-    def pick(dq, dz, sq, sz, off, a, b):
-        op("v", lambda: v.tensor_copy(T[dq][:].bitcast(dt.uint32), T[sq][:].bitcast(dt.uint32).indirect(T[off][:, a:b])), [sq, off], [dq])
-        op("s", lambda: s.activation(T[dz][:], T[sz][:].indirect(T[off][:, a:b]), F.Copy), [sz, off], [dz])
+    def ts(out, in_, s1, s2, o1, o2, r, w):
+        if o2 is None:
+            op("v", lambda: v.tensor_scalar(out, in_, s1, None, o1), r, w)
+        else:
+            op("v", lambda: v.tensor_scalar(out, in_, s1, s2, o1, o2), r, w)
+
+    def quant(q, z, tile, a, b, r, w):
+        op("v", lambda: v.quantize_mx(T[q][:, a:b], T[z][:, a:b], T[tile][:, 4 * a:4 * b]), r, w)
+
+    def pick(dq, dz, sq, sz, off, e, f, c, d, r, w):
+        op("v", lambda: v.tensor_copy(T[dq][:, c:d].bitcast(dt.uint32), T[sq][:].bitcast(dt.uint32).indirect(T[off][:, e:f])), r, [w + "q"])
+        op("s", lambda: s.activation(T[dz][:, c:d], T[sz][:].indirect(T[off][:, e:f]), F.Copy), r, [w + "z"])
 
     dma("y", T.uin[:], T.u[:], [], ["uin"])
     dma("s", T.xin[:, 0:512], T.x[:, 0:512], [], ["xin0"])
     dma("y", T.xin[:, 512:1024], T.x[:, 512:1024], [], ["xin1"])
     dma("s", T.xin[:, 1024:1536], T.x[:, 1024:1536], [], ["xin2"])
-    dma("y", T.wq[:].bitcast(dt.uint8), T.wc[:], [], ["wq"])
-    dma("y", T.wz[:], T.ws[:], [], ["wz"])
+    dma("y", T.wq[:].bitcast(dt.uint8), T.wc[:], [], ["wq0"])
+    dma("y", T.wz[:], T.ws[:], [], ["wz0"])
     dma("y", T.vin[:], T.v[:], [], ["vin"])
 
-    op("p", lambda: g.iota(T.pidx[:], [[0, 1]], 0, 1), [], ["pidx"])
     op("v", lambda: v.memset(T.c32[:], 32.0), [], ["c32"])
-    op("p", lambda: g.affine_select(T.eye[:], T.c32[:], [[-1, 128]], A.is_equal, 0.0, 0, 1), ["c32"], ["eye"])
+    op("p", lambda: g.iota(T.pidx[:], [[0, 1]], 0, 1), [], ["pidx"])
+    op("p", lambda: g.affine_select(T.eye[:], T.c32[:, 0:128], [[-1, 128]], A.is_equal, 0.0, 0, 1), ["c32"], ["eye"])
+    op("p", lambda: g.iota(T.it8[:], [[8, 4]], 0, 0, allow_small_or_imprecise_dtypes=True), [], ["it8"])
     op("v", lambda: v.memset(T.ef[:], 0.0), [], ["ef"])
-    op("v", lambda: v.tensor_scalar(T.pi2[:, 0:1], T.pidx[:], 16, None, A.bitwise_and), ["pidx"], ["pi2a"])
-    op("v", lambda: v.tensor_scalar(T.pi2[:, 1:2], T.pidx[:], 5, None, A.arith_shift_right), ["pidx"], ["pi2b"])
-    op("v", lambda: v.tensor_scalar(T.pf[:, 0:1], T.pi2[:, 0:1], -0.0625, 1.0, A.mult, A.add), ["pi2a"], ["even"])
-    op("v", lambda: v.tensor_scalar(T.pf[:, 1:2], T.pi2[:, 0:1], 0.0625, None, A.mult), ["pi2a"], ["odd"])
-    op("v", lambda: v.tensor_scalar(T.pf[:, 2:3], T.pi2[:, 1:2], 32.0, 15.0, A.mult, A.add), ["pi2b"], ["base0"])
-    op("v", lambda: v.tensor_scalar(T.pf[:, 3:4], T.pi2[:, 1:2], 32.0, 31.0, A.mult, A.add), ["pi2b"], ["base1"])
+    for i, (b, sh) in enumerate(((16, 0), (-1, 5), (15, 1), (1, 0), (6, 0), (8, 3))):
+        if b < 0:
+            ts(T.pi2[:, i:i + 1], T.pidx[:], sh, None, A.arith_shift_right, None, ["pidx"], ["i%d" % i])
+        elif sh:
+            ts(T.pi2[:, i:i + 1], T.pidx[:], b, sh, A.bitwise_and, A.logical_shift_right, ["pidx"], ["i%d" % i])
+        else:
+            ts(T.pi2[:, i:i + 1], T.pidx[:], b, None, A.bitwise_and, None, ["pidx"], ["i%d" % i])
+    for i, (k, m, c) in enumerate(((0, -0.0625, 1.0), (0, 0.0625, 0.0), (1, 32.0, 15.0), (1, 32.0, 31.0), (2, 1.0, 0.0), (3, 32.0, 0.0), (5, 1.0, 0.0))):
+        ts(T.pf[:, i:i + 1], T.pi2[:, k:k + 1], m, c, A.mult, A.add, ["i%d" % k], ["pf%d" % i])
     for b in range(4):
         cp("v", T.ef[:, 512 * b + b:512 * (b + 1):4], T.eye[:], ["eye", "ef"], ["efb%d" % b])
     efk = ["ef"] + ["efb%d" % b for b in range(4)]
-    op("s", lambda: s.activation(T.eo[:], T.ef[:], F.Copy, scale=T.pf[:, 1:2]), efk + ["odd"], ["eo"])
-    op("v", lambda: v.quantize_mx(T.efq[:], T.efz[:], T.ef[:]), efk, ["efq", "efz"])
-    op("v", lambda: v.tensor_scalar(T.ee[:], T.ef[:], T.pf[:, 0:1], None, A.mult), efk + ["even"], ["ee"])
-    op("v", lambda: v.quantize_mx(T.eeq[:], T.eez[:], T.ee[:]), ["ee"], ["eeq", "eez"])
-    op("v", lambda: v.memset(T.cap[:], BIG), [], ["cap"])
-    op("v", lambda: v.memset(T.cap[:, 0:C:16], -BIG), [], ["cap"])
-    op("v", lambda: v.memset(T.ex[:, 0:1], -BIG), [], ["ex"])
-    op("v", lambda: v.memset(T.k32[:], 0.0), [], ["k32"])
-    quant("uq0", "uz0", "uin")
+    op("s", lambda: s.activation(T.codd[:], T.c32[:], F.Copy, scale=T.pf[:, 1:2]), ["c32", "pf1"], ["codd"])
+    for b in range(4):
+        op("p", lambda: g.affine_select(T.eo[:, 512 * b:512 * b + 512], T.codd[:], [[-1, 512]], A.is_equal, 0.0, b, 4), ["codd"], ["eo%d" % b])
+    op("s", lambda: s.activation(T.cap[:], T.ef[:, 0:C], F.Copy, scale=0.0, bias=BIG), efk, ["cap"])
+    op("s", lambda: s.activation(T.ee[:], T.ef[:], F.Copy, scale=T.pf[:, 0:1]), efk + ["pf0"], ["ee"])
+    op("s", lambda: s.activation(T.hist[:, 0:HW], T.ef[:, 0:HW], F.Copy, scale=0.0, bias=BIG), efk, ["h0"])
+    op("s", lambda: s.activation(T.one[:], T.ef[:, 0:C], F.Copy, scale=0.0, bias=1.0), efk, ["one"])
+    op("v", lambda: v.quantize_mx(T.efq[:], T.efz[:], T.ef[:]), efk, ["efq"])
+    quant("uq0", "uz0", "uin", 0, 128, ["uin"], ["U0"])
     for i in range(3):
-        quant("xq0", "xz0", "xin", 128 * i, 128 * i + 128, "xin%d" % i)
-    op("v", lambda: v.quantize_mx(T.eoq[:], T.eoz[:], T.eo[:]), ["eo"], ["eoq", "eoz"])
-    op("v", lambda: v.memset(T.n32[:], 0.0), [], ["n32"])
+        quant("xq0", "xz0", "xin", 128 * i, 128 * i + 128, ["xin%d" % i], ["X00", "X01"] if i == 1 else ["X0%d" % (i // 2)])
+    ts(T.ordk[:], T.it8[:], T.pf[:, 4:5], T.pf[:, 5:6], A.add, A.add, ["it8", "pf4", "pf5"], ["ordk"])
+    ts(T.ordn[:, 0:1], T.pi2[:, 4:5], T.pf[:, 5:6], T.pf[:, 6:7], A.add, A.add, ["i4", "pf5", "pf6"], ["ordn"])
+    op("v", lambda: v.memset(T.ex[:, 0:1], -BIG), [], ["ex0"])
+    op("v", lambda: v.memset(T.k32[:, 24:32], 0.0), [], ["k32z"])
+    op("v", lambda: v.memset(T.n32[:, 8:32], 0.0), [], ["n32z"])
     op("v", lambda: v.memset(T.ones[:], 1.0), [], ["ones"])
-    op("v", lambda: v.memset(T.ep[:], 0.0), [], ["ep"])
-    op("v", lambda: v.memset(T.hist[:, 0:HW], BIG), [], ["h0"])
+    op("v", lambda: v.memset(T.ep[:, 0:1], 0.0), [], ["ep0"])
     op("v", lambda: v.memset(T.hist[:, HW:9 * HW:HW], -BIG), [], ["h%d" % k for k in range(1, 9)])
-
-    ZB, RB, SB = (1, 2, 3, 4), (5, 6, 7, 1), 0
+    op("v", lambda: v.memset(T.cap[:, 0:C:16], -BIG), ["cap"], ["cap"])
+    SB, S2 = 0, 5
+    BANKS = ((1, 2, 3, 4), (6, 7, 0, 5))
 
     def hv(k):
         return T.hist[:, HW * k + C:HW * k + C + 1]
 
+    def sl(name, k):
+        return T[name][:, C * k:C * k + C]
+
+    def counting(dst, src, bias, r, w):
+        j = "junk%d" % (njunk[0] % 3)
+        njunk[0] += 1
+        op("s", lambda: s.activation(T[j][:], src, F.Sign, bias=bias, scale=-1.0, accum_out=dst), r, [j, w])
+
     def top8(rd):
-        S = P[SB][:, 0:C]
-        for k in range(1, 9):
-            op("v", lambda: v.tensor_tensor_scan(T.hist[:, HW * k + 1:HW * k + 1 + C], S, T.hist[:, HW * (k - 1):HW * (k - 1) + C], -BIG, A.max, A.min),
-               ["p0", "h%d" % (k - 1)], ["h%d" % k])
-            if k == 1:
-                yield
+        S = T.ssb[:]
+        todo, ready, done = [], set(), set()
+
+        def move(G):
+            for a in range(4):
+                o, i = T.n32[32 * G:32 * G + 32, 2 * a:2 * a + 2], T.cn[32 * a:32 * a + 32, 2 * G:2 * G + 2]
+                r, w = ["c%d" % (2 * G), "c%d" % (2 * G + 1)], ["n32%d%d" % (G, a)]
+                if G in PAR["dma"]:
+                    dma("y", o, i, r, w, "m%d%d" % (rd, G))
+                else:
+                    cp("v" if a in PAR["vm"] else "s", o, i, r, w)
+            if G in PAR["dma"]:
+                for a in range(3):
+                    lastw["n32%d%d" % (G, a)] = dict(lastw["n32%d3" % G])
+
+        def flush():
+            for i in [i for i in todo if i in ready]:
+                counting(T.cn[:, i:i + 1], sl("cu", i), T.ob[:, i:i + 1], ["q%d" % i, "ob%d" % (i // 4)], "c%d" % i)
+                todo.remove(i)
+                done.add(i)
+                if i == 1 or i % 2 and i - 1 in done or i % 2 == 0 and i + 1 in done:
+                    move(i // 2)
+        for what in PAR["seq"].split():
+            w, k = what[0], int(what[1:])
+            if w == "M":
+                op("v", lambda: v.tensor_tensor_scan(T.hist[:, HW * k + 1:HW * k + 1 + C], S, T.hist[:, HW * (k - 1):HW * (k - 1) + C], -BIG, A.max, A.min),
+                   ["S", "h%d" % (k - 1)], ["h%d" % k])
+                if k == 1:
+                    counting(T.n0[:], T.hist[:, HW + 1:HW + 1 + C], hv(1), ["h1"], "n0")
+            elif w == "E" and k in PAR["ea"] + PAR["eb"]:
+                op("s", lambda: s.activation(sl("sg", k), S, F.Sign, bias=hv(k + 1), scale=-1.0), ["S", "h%d" % (k + 1)], ["s%d" % k])
+                if k in PAR["eb"]:
+                    op("s", lambda: s.activation(sl("fl", k), sl("sg", k), F.Abs), ["s%d" % k], ["f%d" % k])
+                continue
+            elif w == "E":
+                ts(sl("fl", k), S, hv(k + 1), None, A.is_equal, None, ["S", "h%d" % (k + 1)], ["f%d" % k])
+            elif w == "H":
+                if k not in PAR["ea"]:
+                    continue
+                ts(sl("fl", k), sl("sg", k), 0.0, None, A.is_equal, None, ["s%d" % k], ["f%d" % k])
+            elif w == "Q":
+                if k in PAR["eb"]:
+                    op("v", lambda: v.tensor_tensor_scan(sl("cu", k), T.one[:], sl("fl", k), 0.5, A.add, A.subtract), ["f%d" % k, "one"], ["q%d" % k])
+                else:
+                    op("v", lambda: v.tensor_tensor_scan(sl("cu", k), sl("fl", k), sl("fl", k), 0.5, A.add, A.max), ["f%d" % k], ["q%d" % k])
+                todo.append(k)
+                flush()
+            elif w == "O":
+                a, b = (1, 4) if k == 1 else (4, 8)
+                op("v", lambda: v.tensor_tensor(T.ep[:, a:b], T.hist[:, HW * (a + 1) + C:HW * (b + 1):HW], T.hist[:, HW * a + C:HW * b:HW], A.is_equal),
+                   ["h%d" % i for i in range(a, b + 1)], ["ep%d" % k])
+                if k == 1:
+                    ts(T.cn[:, 0:1], T.n0[:], 2.0, -384.0, A.mult, A.add, ["n0"], ["c0"])
             else:
-                yield
-        op("v", lambda: v.tensor_tensor(T.ep[:, 1:8], T.hist[:, 2 * HW + C:9 * HW:HW], T.hist[:, HW + C:8 * HW:HW], A.is_equal),
-           ["h%d" % k for k in range(1, 9)], ["ep"])
-        op("s", lambda: s.activation(T.junk[:], T.hist[:, HW + 1:HW + 1 + C], F.Sign, bias=hv(1), scale=-1.0, accum_out=T.n32[:, 0:1]),
-           ["h1"], ["junk", "n32a"])
-        yield
-        for gg in range(1, 8):
-            op("v", lambda: v.tensor_scalar(T["f%d" % gg][:], S, hv(gg + 1), None, A.is_equal), ["p0", "h%d" % (gg + 1)], ["f%d" % gg])
-            if gg == 1:
-                op("v", lambda: v.tensor_tensor_scan(T.ob[:], T.ep[:], T.ones[:], 0.0, A.mult, A.add), ["ep", "ones"], ["ob"])
-            yield
-            op("v", lambda: v.tensor_tensor_scan(T["q%d" % gg][:], T["f%d" % gg][:], T["f%d" % gg][:], 0.5, A.add, A.max), ["f%d" % gg], ["q%d" % gg])
-            op("s", lambda: s.activation(T.junk[:], T["q%d" % gg][:], F.Sign, bias=T.ob[:, gg:gg + 1], scale=-1.0, accum_out=T.cn[:, gg:gg + 1]),
-               ["q%d" % gg, "ob"], ["junk", "cn"])
+                a, b = (0, 4) if k == 1 else (4, 8)
+                op("v", lambda: v.tensor_tensor_scan(T.ob[:, a:b], T.ep[:, a:b], T.ones[:, a:b], T.ob[:, 3:4] if a else 0.0, A.mult, A.add),
+                   (["ob0", "ep2"] if a else ["ep0", "ep1"]) + ["ones"], ["ob%d" % (k - 1)])
+                ready.update(range(a, b))
+                flush()
             yield
 
-    def spread(src, tb, db, ob):
-        op("v", lambda: v.transpose(T[tb][:], T[src][:]), [src] if src == "k32" else [src, "n32a"], [tb])
+    def spread(src, keys, tb, db, ob, gap):
+        op("v", lambda: v.transpose(T[tb][:], T[src][:]), keys, [tb])
+        gap()
         for i in range(2):
             cp("v", T[db][:, :, i, :], T[tb][:], [tb], [db + str(i)])
+        gap()
         op("v", lambda: v.transpose(T[ob][:], T[db][:]), [db + "0", db + "1"], [ob])
+        gap()
 
     for rd in (1, 2, 3):
         xq, xz, uq, uz = "xq%d" % (rd - 1), "xz%d" % (rd - 1), "uq%d" % (rd - 1), "uz%d" % (rd - 1)
         nq, nz = "xq%d" % rd, "xz%d" % rd
+        uk, xk, nk = ["U%d" % (rd - 1)], ["X%d%d" % (rd - 1, h) for h in (0, 1)], ["X%d%d" % (rd, h) for h in (0, 1)]
+
+        def unpack(bank, h, b):
+            mm(bank, "efq", "efz", 128 * b, xq, xz, HALF[h][0], HALF[h][1], [xk[h]], True, False)
+
+        def ahead():
+            for b in range(4):
+                unpack(BANKS[0][b], 0, b)
+            for b in range(2):
+                unpack(BANKS[1][b], 1, b)
         if rd > 1:
-            for b in range(4):
-                mm(ZB[b], C, "efq", "efz", 128 * b, xq, xz, True, False)
-        mm(SB, C, uq, uz, 0, xq, xz, True, True)
+            ahead()
+        mm(SB, uq, uz, 0, xq, xz, 0, C, uk + xk, True, True)
+        mm(S2, uq, uz, 0, xq, xz, 0, C, uk + xk, True, True)
         if rd == 1:
-            for b in range(4):
-                mm(ZB[b], C, "efq", "efz", 128 * b, xq, xz, True, False)
-        for b in range(3):
-            mm(RB[b], C, "efq", "efz", 128 * b, xq, xz, True, False)
-        op("v", lambda: v.transpose(T.st[:], P[SB][:, 0:C]), ["p0"], ["st"])
-        op("v", lambda: v.tensor_tensor_scan(T.ex[:, 1:C], T.st[:, 0:C - 1], T.cap[:, 1:C], -BIG, A.max, A.min), ["st", "cap"], ["ex"])
-        op("v", lambda: v.tensor_tensor(T.nr[:], T.st[:], T.ex[:], A.is_le), ["st", "ex"], ["nr"])
-        op("v", lambda: v.tensor_tensor_scan(T.tr[:], T.nr[:], T.nr[:], 0.0, A.mult, A.add), ["nr"], ["tr"])
-        for i in range(2):
-            op("v", lambda: v.tensor_scalar(T.k32[:, 12 * i:12 * i + 12], T.tr[:, 15 + 16 * i:C:32], -1.0, T.pf[:, 2 + i:3 + i], A.mult, A.add),
-               ["tr", "base%d" % i], ["k32"])
-        spread("k32", "kt", "kd", "ko")
-        ok = "ok%d" % rd
-        for i in range(2):
-            for hh in range(2):
-                cp("v", T[ok][:, 24 * i + hh:24 * i + 24:2], T.ko[:, hh, 12 * i:12 * i + 12], ["ko"], [ok])
-        pick("aeq%d" % rd, "aez%d" % rd, uq, uz, ok, 0, 24)
-        pick("aoq%d" % rd, "aoz%d" % rd, uq, uz, ok, 24, 48)
-        for b in range(4):
-            mm(ZB[b], C, "eeq", "eez", 128 * b, "aeq%d" % rd, "aez%d" % rd, False, False)
-        for b in range(4):
-            mm(ZB[b], C, "eoq", "eoz", 128 * b, "aoq%d" % rd, "aoz%d" % rd, False, True)
-        for b in range(4):
-            cp("s", T.zt[:, b:4 * C:4], P[ZB[b]][:, 0:C], ["p%d" % ZB[b]], ["zt%d" % b], 1.0 / 64)
+            ahead()
         fill = top8(rd)
-        for i in range(7):
-            next(fill, None)
-        mm(RB[3], C, "efq", "efz", 384, xq, xz, True, False)
-        op("v", lambda: v.quantize_mx(T["zq%d" % rd][:], T["zz%d" % rd][:], T.zt[:]), ["zt%d" % b for b in range(4)], ["zq%d" % rd, "zz%d" % rd])
-        for b in range(4):
-            mm(RB[b], C, "wq", "wz", 128 * b, "zq%d" % rd, "zz%d" % rd, False, True)
-        for b in range(4):
-            cp("s", T.xt[:, b:4 * C:4], P[RB[b]][:, 0:C], ["p%d" % RB[b]], ["xt%d" % b], 1.0 / 32)
-        for i in range(9):
-            next(fill, None)
-        op("v", lambda: v.quantize_mx(T[nq][:], T[nz][:], T.xt[:]), ["xt%d" % b for b in range(4)], [nq, nz])
-        for _ in fill:
-            pass
-        if rd == 3:
-            quant("vq", "vz", "vin")
-            mm(5, C, "vq", "vz", 0, nq, nz, True, True)
-        op("v", lambda: v.tensor_scalar(T.n32[:, 1:8], T.cn[:, 1:8], 0.5, 192.0, A.mult, A.add), ["cn"], ["n32"])
-        spread("n32", "nt", "nd", "no")
-        for a in range(4):
-            for G in range(4):
-                cp("v" if (a + G) % 2 else "s", T.xn[32 * G:32 * G + 32, a, :, :], T.no[32 * a:32 * a + 32, :, 2 * G:2 * G + 2], ["no"], ["xn%d%d" % (a, G)])
-        on = "on%d" % rd
+        slots = iter(PAR["down"])
+
+        def gap(n=None):
+            n = next(slots, 0) if n is None else n
+            for _ in range(n):
+                next(fill, None)
+        op("v", lambda: v.transpose(T.st[:], P[SB][:, 0:C]), ["p%d" % SB], ["st"])
+        cp("s", T.ssb[:], P[S2][:, 0:C], ["p%d" % S2], ["S"])
+        for b in (2, 3):
+            unpack(BANKS[1][b], 1, b)
+        gap()
+        op("v", lambda: v.tensor_tensor_scan(T.ex[:, 1:C], T.st[:, 0:C - 1], T.cap[:, 1:C], -BIG, A.max, A.min), ["st", "cap"], ["ex"])
+        gap()
+        op("v", lambda: v.tensor_tensor(T.nr[:], T.st[:], T.ex[:], A.is_le), ["st", "ex", "ex0"], ["nr"])
+        gap()
+        if rd == 1:
+            op("v", lambda: v.quantize_mx(T.eeq[:], T.eez[:], T.ee[:]), ["ee"], ["eeq"])
+        op("v", lambda: v.tensor_tensor_scan(T.tr[:], T.nr[:], T.nr[:], 0.0, A.mult, A.add), ["nr"], ["tr"])
+        gap()
         for i in range(2):
-            cp("v", T[on][:, 8 * i:8 * i + 8], T.xn[:, :, :, i], ["xn%d%d" % (a, G) for a in range(4) for G in range(4)], [on])
-        pick("veq%d" % rd, "vez%d" % rd, nq, nz, on, 0, 8)
-        pick("voq%d" % rd, "voz%d" % rd, nq, nz, on, 8, 16)
+            ts(T.k32[:, 12 * i:12 * i + 12], T.tr[:, 15 + 16 * i:C:32], -1.0, T.pf[:, 2 + i:3 + i], A.mult, A.add, ["tr", "pf%d" % (2 + i)], ["k32%d" % i])
+        gap()
+        spread("k32", ["k320", "k321", "k32z"], "kt", "kd", "ko", gap)
+        if rd == 1:
+            op("v", lambda: v.quantize_mx(T.eoq[:], T.eoz[:], T.eo[:]), ["eo%d" % b for b in range(4)], ["eoq"])
+        op("v", lambda: v.tensor_copy(T.ok[:], T.ko[:].indirect(T.ordk[:, 0:3])), ["ko", "ordk"], ["ok"])
+        gap()
+        for h, (c, d) in enumerate(HALF):
+            for i, e in enumerate("eo"):
+                pick("a%sq%d" % (e, rd), "a%sz%d" % (e, rd), uq, uz, "ok", 24 * i + c // 16, 24 * i + d // 16, c, d, uk + ["ok"], "a%s%d" % (e, h))
+                for b in range(4):
+                    mm(BANKS[h][b], "e%sq" % e, "e%sz" % e, 128 * b, "a%sq%d" % (e, rd), "a%sz%d" % (e, rd), c, d, ["a%s%dq" % (e, h), "a%s%dz" % (e, h)], False, e == "o")
+        for h, (c, d) in enumerate(HALF):
+            def take(q, b):
+                cp(q, T.zt[:, 4 * c + b:4 * d:4], P[BANKS[h][b]][:, 0:d - c], ["p%d" % BANKS[h][b]], ["zt%d%d" % (h, b)], 1.0 / 64)
+            for b in range(4):
+                if b not in PAR["zv"]:
+                    take("s", b)
+            gap(PAR["z"][h])
+            for b in PAR["zv"]:
+                take("v", b)
+            for b in range(4):
+                unpack(BANKS[h][b], h, b)
+            quant("zq", "zz", "zt", c, d, ["zt%d%d" % (h, b) for b in range(4)], ["Z%d" % h])
+            for b in range(4):
+                mm(BANKS[h][b], "wq", "wz", 128 * b, "zq", "zz", c, d, ["Z%d" % h, "wq0", "wz0"], False, True)
+        for h, (c, d) in enumerate(HALF):
+            def give(q, b):
+                cp(q, T.xt[:, 4 * c + b:4 * d:4], P[BANKS[h][b]][:, 0:d - c], ["p%d" % BANKS[h][b]], ["xt%d%d" % (h, b)], 1.0 / 32)
+            for b in range(4):
+                if b not in PAR["xv"]:
+                    give("s", b)
+            gap(PAR["x"][h])
+            for b in PAR["xv"]:
+                give("v", b)
+            quant(nq, nz, "xt", c, d, ["xt%d%d" % (h, b) for b in range(4)], [nk[h]])
+        gap(99)
+        spread("n32", ["n32z"] + ["n32%d%d" % (G, a) for G in range(4) for a in range(4)], "nt", "nd", "no", lambda: None)
+        on = "on%d" % rd
+        ts(T[on][:], T.no[:].indirect(T.ordn[:, 0:1]), 0.5, 192.0, A.mult, A.add, ["no", "ordn"], [on])
+        for i, e in enumerate("eo"):
+            pick("v%sq%d" % (e, rd), "v%sz%d" % (e, rd), nq, nz, on, 8 * i, 8 * i + 8, 0, 128, nk + [on], "v" + e)
+            for b in range(4):
+                mm(BANKS[0][b], "e%sq" % e, "e%sz" % e, 128 * b, "v%sq%d" % (e, rd), "v%sz%d" % (e, rd), 0, 128, ["v%sq" % e, "v%sz" % e], e == "e", e == "o")
         for b in range(4):
-            mm(ZB[b], 128, "eeq", "eez", 128 * b, "veq%d" % rd, "vez%d" % rd, True, False)
-        for b in range(4):
-            mm(ZB[b], 128, "eoq", "eoz", 128 * b, "voq%d" % rd, "voz%d" % rd, False, True)
-        for b in range(4):
-            cp("vs"[b % 2], T.vt[:, b:512:4], P[ZB[b]][:, 0:128], ["p%d" % ZB[b]], ["vt%d" % b], 1.0 / 32)
-        op("v", lambda: v.quantize_mx(T["sq%d" % rd][:], T["sz%d" % rd][:], T.vt[:]), ["vt%d" % b for b in range(4)], ["sq%d" % rd, "sz%d" % rd])
+            cp("vs"[b % 2], T.vt[:, b:512:4], P[BANKS[0][b]][:, 0:128], ["p%d" % BANKS[0][b]], ["vt%d" % b], 1.0 / 32)
+        quant("sq%d" % rd, "sz%d" % rd, "vt", 0, 128, ["vt%d" % b for b in range(4)], ["out"])
         dst = T.cores[(rank + STEP[rd - 1]) % N]
         rid, pid, _ = topo.addr(dst)
         eng = topo.engines(core, dst)
         half = len(eng) // 2
         m1 = sum(1 << e for e in eng[:half])
         m2 = sum(1 << e for e in eng[half:])
-        before("p", ["sq%d" % rd, "sz%d" % rd], [])
+        before("p", ["out"], [])
         g.remote_dma(T["uq%d" % rd][:].bitcast(dt.uint8), T["sq%d" % rd][:].bitcast(dt.uint8), T.sem["rc%d" % rd], T.sem["sent"], pid, rid, m1)
         g.remote_dma(T["uz%d" % rd][:], T["sz%d" % rd][:], T.sem["rc%d" % rd], T.sem["sent"], pid, rid, m2)
         count["sent"] = count.get("sent", 0) + len(eng)
         count["rc%d" % rd] = len(eng)
-        for k in ("uq%d" % rd, "uz%d" % rd):
-            lastw[k] = {"rc%d" % rd: len(eng)}
+        lastw["U%d" % rd] = {"rc%d" % rd: len(eng)}
 
-    cp("s", T.yt[:], P[5][:, 0:C], ["p5"], ["yt"])
-    dma("y", T.oc[:], T.xq3[:].bitcast(dt.uint8), ["xq3"], [], "outy")
+    op("v", lambda: v.quantize_mx(T.vq[:], T.vz[:], T.vin[:]), ["vin"], ["vq"])
+    mm(S2, "vq", "vz", 0, "xq3", "xz3", 0, C, nk, True, True)
+    cp("s", T.yt[:], P[S2][:, 0:C], ["p%d" % S2], ["yt"])
+    ts(T.nop[:], T.nt[:], 0.5, 192.0, A.mult, A.add, ["nt"], ["nop"])
+    dma("y", T.oc[:], T.xq3[:].bitcast(dt.uint8), nk, [], "outy")
     for k in range(4):
-        dma("y", T.osc[4 * k:4 * k + 4, :], T.xz3[32 * k:32 * k + 4, :], ["xz3"], [], "outy")
+        dma("y", T.osc[4 * k:4 * k + 4, :], T.xz3[32 * k:32 * k + 4, :], nk, [], "outy")
     for a in range(4):
         dma("y", T.op[2 * a:2 * a + 2, 0:C], T.kt[32 * a:32 * a + 24, :, :], ["kt"], [], "outy")
-        dma("y", T.op[0:8, C + 32 * a:C + 32 * a + 32], T.nt[32 * a:32 * a + 8, :, :], ["nt"], [], "outy")
     dma("s", T.y[:], T.yt[:], ["yt"], [], "outs")
-    dma("s", T.uc[:], T.uq3[:].bitcast(dt.uint8), ["uq3"], [], "outs")
+    for a in range(4):
+        for i in range(2):
+            dma("y" if i else "s", T.op[2 * a + i, C:C + 128], T.nop[32 * a + i:32 * a + 8:2, :, :], ["nop"], [], "outy" if i else "outs")
+    dma("s", T.uc[:], T.uq3[:].bitcast(dt.uint8), ["U3"], [], "outs")
     for k in range(4):
-        dma("y" if k % 2 else "s", T.usc[4 * k:4 * k + 4, :], T.uz3[32 * k:32 * k + 4, :], ["uz3"], [], "outy" if k % 2 else "outs")
+        dma("y" if k % 2 else "s", T.usc[4 * k:4 * k + 4, :], T.uz3[32 * k:32 * k + 4, :], ["U3"], [], "outy" if k % 2 else "outs")
     for sem in sorted(count):
         wait("p", (sem, count[sem]))

@@ -3,8 +3,8 @@ from concourse.mybir import dt, AluOpType as A, ActivationFunctionType as F
 N, C, U, STEP = 4, 384, 128, (1, 2, 3)
 BIG = 1e29
 HW = 388
-PAR = {"down": (0, 1, 1, 1, 1, 0, 1, 0, 1), "z": (5, 4), "x": (12, 0), "zv": (), "xv": (2, 3), "dma": (0, 1), "vm": (), "ea": (3, 5), "eb": (1, 2),
-       "seq": "M1 M2 E1 M3 M4 M5 E2 E3 O1 H2 H1 B1 H3 M6 E5 Q3 E4 M7 H4 Q2 M8 O2 Q1 H5 B2 Q4 Q5 E7 E6 H6 H7 Q7 Q6"}
+PAR = {"down": (0, 1, 1, 1, 1, 1, 1, 2), "z": (6, 3), "x": (19, 5), "zv": (), "xv": (), "dma": (0, 1), "vm": (0, 1), "ea": (1, 3, 4), "eb": (2,),
+       "seq": "M1 M2 E1 M3 M4 O1 M5 H1 E2 E3 B1 M6 H3 E4 Q1 M7 H2 E5 M8 Q3 H5 Q2 H4 E7 O2 H7 Q5 Q7 B2 E6 H6 Q6 Q4"}
 HALF = ((0, 192), (192, 384))
 
 
@@ -22,8 +22,8 @@ SCRATCH = {
     "eoq": _sb(512, CODE), "eoz": _sb(512, PL),
     "cap": _sb(C, F32), "ones": _sb(8, F32), "one": _sb(C, BF), "ssb": _sb(C, F32),
     "st": _sb(C, F32), "ex": _sb(C, F32), "nr": _sb(C, BF), "tr": _sb(C, BF),
-    "k32": _sb(32, F32), "kt": ("sbuf", [128, 2, 16], F32), "kd": ("sbuf", [128, 2, 2, 16], F32), "ko": _sb(64, F32),
-    "n32": _sb(32, F32), "nt": ("sbuf", [128, 2, 16], F32), "nd": ("sbuf", [128, 2, 2, 16], F32), "no": _sb(64, F32),
+    "k32": _sb(32, F32), "kd": ("sbuf", [128, 2, 2, 16], F32), "ko": _sb(64, F32),
+    "n32": _sb(32, F32), "nd": ("sbuf", [128, 2, 2, 16], F32), "no": _sb(64, F32),
     "nop": ("sbuf", [128, 2, 16], F32), "cn": _sb(8, F32), "n0": _sb(1, F32), "it8": _sb(4, F32), "ordk": _sb(4, U16), "ordn": _sb(2, U16),
     "hist": _sb(9 * HW, F32), "ep": _sb(8, F32), "ob": _sb(8, F32), "sg": _sb(8 * C, BF), "fl": _sb(8 * C, BF), "cu": _sb(8 * C, BF),
     "junk0": _sb(C, BF), "junk1": _sb(C, BF), "junk2": _sb(C, BF),
@@ -183,9 +183,16 @@ def rank_program(g, core, T, topo):
         njunk[0] += 1
         op("s", lambda: s.activation(T[j][:], src, F.Sign, bias=bias, scale=-1.0, accum_out=dst), r, [j, w])
 
+    def spread(src, keys, db, ob):
+        for i in range(2):
+            op("v", lambda: v.transpose(T[db][:, :, i, :], T[src][:]), keys, [db + str(i)])
+        yield
+        op("v", lambda: v.transpose(T[ob][:], T[db][:]), [db + "0", db + "1"], [ob])
+        yield
+
     def top8(rd):
         S = T.ssb[:]
-        todo, ready, done = [], set(), set()
+        todo, ready, done, late = [], set(), set(), []
 
         def move(G):
             for a in range(4):
@@ -204,8 +211,12 @@ def rank_program(g, core, T, topo):
                 counting(T.cn[:, i:i + 1], sl("cu", i), T.ob[:, i:i + 1], ["q%d" % i, "ob%d" % (i // 4)], "c%d" % i)
                 todo.remove(i)
                 done.add(i)
+                while late:
+                    move(late.pop())
                 if i == 1 or i % 2 and i - 1 in done or i % 2 == 0 and i + 1 in done:
-                    move(i // 2)
+                    late.append(i // 2)
+                    if i // 2 in PAR["dma"]:
+                        move(late.pop())
         for what in PAR["seq"].split():
             w, k = what[0], int(what[1:])
             if w == "M":
@@ -244,19 +255,17 @@ def rank_program(g, core, T, topo):
                 ready.update(range(a, b))
                 flush()
             yield
-
-    def spread(src, keys, tb, db, ob, gap):
-        op("v", lambda: v.transpose(T[tb][:], T[src][:]), keys, [tb])
-        gap()
-        for i in range(2):
-            cp("v", T[db][:, :, i, :], T[tb][:], [tb], [db + str(i)])
-        gap()
-        op("v", lambda: v.transpose(T[ob][:], T[db][:]), [db + "0", db + "1"], [ob])
-        gap()
+        while late:
+            move(late.pop())
+        for _ in spread("n32", ["n32z"] + ["n32%d%d" % (G, a) for G in range(4) for a in range(4)], "nd", "no"):
+            yield
+        on = "on%d" % rd
+        ts(T[on][:], T.no[:].indirect(T.ordn[:, 0:1]), 0.5, 192.0, A.mult, A.add, ["no", "ordn"], [on])
+        yield
 
     for rd in (1, 2, 3):
         xq, xz, uq, uz = "xq%d" % (rd - 1), "xz%d" % (rd - 1), "uq%d" % (rd - 1), "uz%d" % (rd - 1)
-        nq, nz = "xq%d" % rd, "xz%d" % rd
+        nq, nz, on = "xq%d" % rd, "xz%d" % rd, "on%d" % rd
         uk, xk, nk = ["U%d" % (rd - 1)], ["X%d%d" % (rd - 1, h) for h in (0, 1)], ["X%d%d" % (rd, h) for h in (0, 1)]
 
         def unpack(bank, h, b):
@@ -296,7 +305,8 @@ def rank_program(g, core, T, topo):
         for i in range(2):
             ts(T.k32[:, 12 * i:12 * i + 12], T.tr[:, 15 + 16 * i:C:32], -1.0, T.pf[:, 2 + i:3 + i], A.mult, A.add, ["tr", "pf%d" % (2 + i)], ["k32%d" % i])
         gap()
-        spread("k32", ["k320", "k321", "k32z"], "kt", "kd", "ko", gap)
+        for _ in spread("k32", ["k320", "k321", "k32z"], "kd", "ko"):
+            gap()
         if rd == 1:
             op("v", lambda: v.quantize_mx(T.eoq[:], T.eoz[:], T.eo[:]), ["eo%d" % b for b in range(4)], ["eoq"])
         op("v", lambda: v.tensor_copy(T.ok[:], T.ko[:].indirect(T.ordk[:, 0:3])), ["ko", "ordk"], ["ok"])
@@ -331,9 +341,6 @@ def rank_program(g, core, T, topo):
                 give("v", b)
             quant(nq, nz, "xt", c, d, ["xt%d%d" % (h, b) for b in range(4)], [nk[h]])
         gap(99)
-        spread("n32", ["n32z"] + ["n32%d%d" % (G, a) for G in range(4) for a in range(4)], "nt", "nd", "no", lambda: None)
-        on = "on%d" % rd
-        ts(T[on][:], T.no[:].indirect(T.ordn[:, 0:1]), 0.5, 192.0, A.mult, A.add, ["no", "ordn"], [on])
         for i, e in enumerate("eo"):
             pick("v%sq%d" % (e, rd), "v%sz%d" % (e, rd), nq, nz, on, 8 * i, 8 * i + 8, 0, 128, nk + [on], "v" + e)
             for b in range(4):
@@ -357,12 +364,12 @@ def rank_program(g, core, T, topo):
     op("v", lambda: v.quantize_mx(T.vq[:], T.vz[:], T.vin[:]), ["vin"], ["vq"])
     mm(S2, "vq", "vz", 0, "xq3", "xz3", 0, C, nk, True, True)
     cp("s", T.yt[:], P[S2][:, 0:C], ["p%d" % S2], ["yt"])
-    ts(T.nop[:], T.nt[:], 0.5, 192.0, A.mult, A.add, ["nt"], ["nop"])
+    ts(T.nop[:], T.nd[:, :, 0, :], 0.5, 192.0, A.mult, A.add, ["nd0"], ["nop"])
     dma("y", T.oc[:], T.xq3[:].bitcast(dt.uint8), nk, [], "outy")
     for k in range(4):
         dma("y", T.osc[4 * k:4 * k + 4, :], T.xz3[32 * k:32 * k + 4, :], nk, [], "outy")
     for a in range(4):
-        dma("y", T.op[2 * a:2 * a + 2, 0:C], T.kt[32 * a:32 * a + 24, :, :], ["kt"], [], "outy")
+        dma("y", T.op[2 * a:2 * a + 2, 0:C], T.kd[32 * a:32 * a + 24, :, 0, :], ["kd0"], [], "outy")
     dma("s", T.y[:], T.yt[:], ["yt"], [], "outs")
     for a in range(4):
         for i in range(2):

from concourse.mybir import dt, AluOpType as A, ActivationFunctionType as F

N, C, U, STEP = 4, 384, 128, (1, 2, 3)
BIG = 1e29
HW = 388
PAR = {"down": (0, 1, 1, 1, 1, 1, 1, 2), "z": (6, 3), "x": (19, 5), "zv": (), "xv": (), "dma": (0, 1), "vm": (0, 1), "ea": (1, 3, 4), "eb": (2,),
       "seq": "M1 M2 E1 M3 M4 O1 M5 H1 E2 E3 B1 M6 H3 E4 Q1 M7 H2 E5 M8 Q3 H5 Q2 H4 E7 O2 H7 Q5 Q7 B2 E6 H6 Q6 Q4"}
HALF = ((0, 192), (192, 384))


def _sb(n, d):
    return ("sbuf", [128, n], d)


CODE, PL, BF, F32, U16, I32 = "float8_e4m3fn_x4", "uint8", "bfloat16", "float32", "uint16", "int32"
SCRATCH = {
    "xin": _sb(4 * C, BF), "uin": _sb(512, BF), "vin": _sb(512, BF),
    "wq": _sb(512, CODE), "wz": _sb(512, PL), "vq": _sb(128, CODE), "vz": _sb(128, PL),
    "c32": _sb(512, BF), "codd": _sb(512, BF), "eye": _sb(128, BF), "pidx": _sb(1, I32), "pi2": _sb(6, I32), "pf": _sb(8, F32),
    "ef": _sb(2048, BF), "ee": _sb(2048, BF), "eo": _sb(2048, BF),
    "efq": _sb(512, CODE), "efz": _sb(512, PL), "eeq": _sb(512, CODE), "eez": _sb(512, PL),
    "eoq": _sb(512, CODE), "eoz": _sb(512, PL),
    "cap": _sb(C, F32), "ones": _sb(8, F32), "one": _sb(C, BF), "ssb": _sb(C, F32),
    "st": _sb(C, F32), "ex": _sb(C, F32), "nr": _sb(C, BF), "tr": _sb(C, BF),
    "k32": _sb(32, F32), "kd": ("sbuf", [128, 2, 2, 16], F32), "ko": _sb(64, F32),
    "n32": _sb(32, F32), "nd": ("sbuf", [128, 2, 2, 16], F32), "no": _sb(64, F32),
    "nop": ("sbuf", [128, 2, 16], F32), "cn": _sb(8, F32), "n0": _sb(1, F32), "it8": _sb(4, F32), "ordk": _sb(4, U16), "ordn": _sb(2, U16),
    "hist": _sb(9 * HW, F32), "ep": _sb(8, F32), "ob": _sb(8, F32), "sg": _sb(8 * C, BF), "fl": _sb(8 * C, BF), "cu": _sb(8 * C, BF),
    "junk0": _sb(C, BF), "junk1": _sb(C, BF), "junk2": _sb(C, BF),
    "zt": _sb(4 * C, BF), "xt": _sb(4 * C, BF), "vt": _sb(512, BF), "yt": _sb(C, F32),
    "xq0": _sb(C, CODE), "xz0": _sb(C, PL), "uq0": _sb(128, CODE), "uz0": _sb(128, PL),
    "zq": _sb(C, CODE), "zz": _sb(C, PL), "ok": _sb(48, U16)}
for _h in (1, 2, 3):
    SCRATCH.update({
        "xq%d" % _h: _sb(C, CODE), "xz%d" % _h: _sb(C, PL), "uq%d" % _h: _sb(128, CODE), "uz%d" % _h: _sb(128, PL),
        "aeq%d" % _h: _sb(C, CODE), "aez%d" % _h: _sb(C, PL), "aoq%d" % _h: _sb(C, CODE), "aoz%d" % _h: _sb(C, PL),
        "veq%d" % _h: _sb(128, CODE), "vez%d" % _h: _sb(128, PL), "voq%d" % _h: _sb(128, CODE), "voz%d" % _h: _sb(128, PL),
        "sq%d" % _h: _sb(128, CODE), "sz%d" % _h: _sb(128, PL), "on%d" % _h: _sb(16, U16)})
for _b in range(8):
    SCRATCH["p%d" % _b] = ("psum", [128, 512], F32)

SEMAPHORES = (["cv", "cs", "ct", "cp", "sent", "rc1", "rc2", "rc3", "outy", "outs"] + ["d%d" % i for i in range(12)]
              + ["m%d%d" % (h, i) for h in (1, 2, 3) for i in range(4)])


def rank_program(g, core, T, topo):
    rank = T.rank_of(core)
    if rank is None:
        return
    queues = {"v": g.vector, "s": g.scalar, "t": g.tensor, "p": g, "y": g.sync}
    count, seen, lastw, readers, nd, njunk = {}, {q: {} for q in queues}, {}, {}, [0], [0]

    def wait(qn, tok):
        sem, val = tok
        if seen[qn].get(sem, 0) < val:
            queues[qn].wait_ge(T.sem[sem], val)
            seen[qn][sem] = val

    def before(qn, r, w):
        need = {}
        own = "c" + qn
        for k in r:
            for s, v in lastw.get(k, {}).items():
                need[s] = max(need.get(s, 0), v)
        for k in w:
            for s, v in lastw.get(k, {}).items():
                if not (qn == "t" and s == own):
                    need[s] = max(need.get(s, 0), v)
            for s, v in readers.get(k, {}).items():
                if s != own:
                    need[s] = max(need.get(s, 0), v)
        for s in sorted(need):
            wait(qn, (s, need[s]))

    def after(tok, r, w):
        for k in w:
            lastw[k] = {tok[0]: tok[1]}
            readers[k] = {}
        for k in r:
            readers.setdefault(k, {})[tok[0]] = tok[1]

    def op(qn, f, r, w):
        before(qn, r, w)
        sem = "c" + qn
        count[sem] = count.get(sem, 0) + 1
        f().then_inc(T.sem[sem], 1)
        after((sem, count[sem]), r, w)

    def dma(qn, out, in_, r, w, sem=None):
        before(qn, r, w)
        if sem is None:
            sem = "d%d" % nd[0]
            nd[0] += 1
        count[sem] = count.get(sem, 0) + 16
        queues[qn].dma_start(out, in_).then_inc(T.sem[sem], 16)
        after((sem, count[sem]), r, w)

    v, s, t = g.vector, g.scalar, g.tensor
    P = [T["p%d" % b] for b in range(8)]

    def mm(bank, lq, lz, a, rq, rz, c, d, keys, start, stop):
        op("t", lambda: t.matmul_mx(P[bank][:, 0:d - c], T[lq][:, a:a + 128], T[lz][:, a:a + 128], T[rq][:, c:d], T[rz][:, c:d], start, stop),
           [lq] + keys, ["p%d" % bank])

    def cp(qn, out, in_, r, w, scale=None):
        if qn == "v":
            if scale is None:
                op("v", lambda: v.tensor_copy(out, in_), r, w)
            else:
                op("v", lambda: v.tensor_scalar(out, in_, scale, None, A.mult), r, w)
        else:
            op("s", lambda: s.activation(out, in_, F.Copy, scale=1.0 if scale is None else scale), r, w)

    def ts(out, in_, s1, s2, o1, o2, r, w):
        if o2 is None:
            op("v", lambda: v.tensor_scalar(out, in_, s1, None, o1), r, w)
        else:
            op("v", lambda: v.tensor_scalar(out, in_, s1, s2, o1, o2), r, w)

    def quant(q, z, tile, a, b, r, w):
        op("v", lambda: v.quantize_mx(T[q][:, a:b], T[z][:, a:b], T[tile][:, 4 * a:4 * b]), r, w)

    def pick(dq, dz, sq, sz, off, e, f, c, d, r, w):
        op("v", lambda: v.tensor_copy(T[dq][:, c:d].bitcast(dt.uint32), T[sq][:].bitcast(dt.uint32).indirect(T[off][:, e:f])), r, [w + "q"])
        op("s", lambda: s.activation(T[dz][:, c:d], T[sz][:].indirect(T[off][:, e:f]), F.Copy), r, [w + "z"])

    dma("y", T.uin[:], T.u[:], [], ["uin"])
    dma("s", T.xin[:, 0:512], T.x[:, 0:512], [], ["xin0"])
    dma("y", T.xin[:, 512:1024], T.x[:, 512:1024], [], ["xin1"])
    dma("s", T.xin[:, 1024:1536], T.x[:, 1024:1536], [], ["xin2"])
    dma("y", T.wq[:].bitcast(dt.uint8), T.wc[:], [], ["wq0"])
    dma("y", T.wz[:], T.ws[:], [], ["wz0"])
    dma("y", T.vin[:], T.v[:], [], ["vin"])

    op("v", lambda: v.memset(T.c32[:], 32.0), [], ["c32"])
    op("p", lambda: g.iota(T.pidx[:], [[0, 1]], 0, 1), [], ["pidx"])
    op("p", lambda: g.affine_select(T.eye[:], T.c32[:, 0:128], [[-1, 128]], A.is_equal, 0.0, 0, 1), ["c32"], ["eye"])
    op("p", lambda: g.iota(T.it8[:], [[8, 4]], 0, 0, allow_small_or_imprecise_dtypes=True), [], ["it8"])
    op("v", lambda: v.memset(T.ef[:], 0.0), [], ["ef"])
    for i, (b, sh) in enumerate(((16, 0), (-1, 5), (15, 1), (1, 0), (6, 0), (8, 3))):
        if b < 0:
            ts(T.pi2[:, i:i + 1], T.pidx[:], sh, None, A.arith_shift_right, None, ["pidx"], ["i%d" % i])
        elif sh:
            ts(T.pi2[:, i:i + 1], T.pidx[:], b, sh, A.bitwise_and, A.logical_shift_right, ["pidx"], ["i%d" % i])
        else:
            ts(T.pi2[:, i:i + 1], T.pidx[:], b, None, A.bitwise_and, None, ["pidx"], ["i%d" % i])
    for i, (k, m, c) in enumerate(((0, -0.0625, 1.0), (0, 0.0625, 0.0), (1, 32.0, 15.0), (1, 32.0, 31.0), (2, 1.0, 0.0), (3, 32.0, 0.0), (5, 1.0, 0.0))):
        ts(T.pf[:, i:i + 1], T.pi2[:, k:k + 1], m, c, A.mult, A.add, ["i%d" % k], ["pf%d" % i])
    for b in range(4):
        cp("v", T.ef[:, 512 * b + b:512 * (b + 1):4], T.eye[:], ["eye", "ef"], ["efb%d" % b])
    efk = ["ef"] + ["efb%d" % b for b in range(4)]
    op("s", lambda: s.activation(T.codd[:], T.c32[:], F.Copy, scale=T.pf[:, 1:2]), ["c32", "pf1"], ["codd"])
    for b in range(4):
        op("p", lambda: g.affine_select(T.eo[:, 512 * b:512 * b + 512], T.codd[:], [[-1, 512]], A.is_equal, 0.0, b, 4), ["codd"], ["eo%d" % b])
    op("s", lambda: s.activation(T.cap[:], T.ef[:, 0:C], F.Copy, scale=0.0, bias=BIG), efk, ["cap"])
    op("s", lambda: s.activation(T.ee[:], T.ef[:], F.Copy, scale=T.pf[:, 0:1]), efk + ["pf0"], ["ee"])
    op("s", lambda: s.activation(T.hist[:, 0:HW], T.ef[:, 0:HW], F.Copy, scale=0.0, bias=BIG), efk, ["h0"])
    op("s", lambda: s.activation(T.one[:], T.ef[:, 0:C], F.Copy, scale=0.0, bias=1.0), efk, ["one"])
    op("v", lambda: v.quantize_mx(T.efq[:], T.efz[:], T.ef[:]), efk, ["efq"])
    quant("uq0", "uz0", "uin", 0, 128, ["uin"], ["U0"])
    for i in range(3):
        quant("xq0", "xz0", "xin", 128 * i, 128 * i + 128, ["xin%d" % i], ["X00", "X01"] if i == 1 else ["X0%d" % (i // 2)])
    ts(T.ordk[:], T.it8[:], T.pf[:, 4:5], T.pf[:, 5:6], A.add, A.add, ["it8", "pf4", "pf5"], ["ordk"])
    ts(T.ordn[:, 0:1], T.pi2[:, 4:5], T.pf[:, 5:6], T.pf[:, 6:7], A.add, A.add, ["i4", "pf5", "pf6"], ["ordn"])
    op("v", lambda: v.memset(T.ex[:, 0:1], -BIG), [], ["ex0"])
    op("v", lambda: v.memset(T.k32[:, 24:32], 0.0), [], ["k32z"])
    op("v", lambda: v.memset(T.n32[:, 8:32], 0.0), [], ["n32z"])
    op("v", lambda: v.memset(T.ones[:], 1.0), [], ["ones"])
    op("v", lambda: v.memset(T.ep[:, 0:1], 0.0), [], ["ep0"])
    op("v", lambda: v.memset(T.hist[:, HW:9 * HW:HW], -BIG), [], ["h%d" % k for k in range(1, 9)])
    op("v", lambda: v.memset(T.cap[:, 0:C:16], -BIG), ["cap"], ["cap"])
    SB, S2 = 0, 5
    BANKS = ((1, 2, 3, 4), (6, 7, 0, 5))

    def hv(k):
        return T.hist[:, HW * k + C:HW * k + C + 1]

    def sl(name, k):
        return T[name][:, C * k:C * k + C]

    def counting(dst, src, bias, r, w):
        j = "junk%d" % (njunk[0] % 3)
        njunk[0] += 1
        op("s", lambda: s.activation(T[j][:], src, F.Sign, bias=bias, scale=-1.0, accum_out=dst), r, [j, w])

    def spread(src, keys, db, ob):
        for i in range(2):
            op("v", lambda: v.transpose(T[db][:, :, i, :], T[src][:]), keys, [db + str(i)])
        yield
        op("v", lambda: v.transpose(T[ob][:], T[db][:]), [db + "0", db + "1"], [ob])
        yield

    def top8(rd):
        S = T.ssb[:]
        todo, ready, done, late = [], set(), set(), []

        def move(G):
            for a in range(4):
                o, i = T.n32[32 * G:32 * G + 32, 2 * a:2 * a + 2], T.cn[32 * a:32 * a + 32, 2 * G:2 * G + 2]
                r, w = ["c%d" % (2 * G), "c%d" % (2 * G + 1)], ["n32%d%d" % (G, a)]
                if G in PAR["dma"]:
                    dma("y", o, i, r, w, "m%d%d" % (rd, G))
                else:
                    cp("v" if a in PAR["vm"] else "s", o, i, r, w)
            if G in PAR["dma"]:
                for a in range(3):
                    lastw["n32%d%d" % (G, a)] = dict(lastw["n32%d3" % G])

        def flush():
            for i in [i for i in todo if i in ready]:
                counting(T.cn[:, i:i + 1], sl("cu", i), T.ob[:, i:i + 1], ["q%d" % i, "ob%d" % (i // 4)], "c%d" % i)
                todo.remove(i)
                done.add(i)
                while late:
                    move(late.pop())
                if i == 1 or i % 2 and i - 1 in done or i % 2 == 0 and i + 1 in done:
                    late.append(i // 2)
                    if i // 2 in PAR["dma"]:
                        move(late.pop())
        for what in PAR["seq"].split():
            w, k = what[0], int(what[1:])
            if w == "M":
                op("v", lambda: v.tensor_tensor_scan(T.hist[:, HW * k + 1:HW * k + 1 + C], S, T.hist[:, HW * (k - 1):HW * (k - 1) + C], -BIG, A.max, A.min),
                   ["S", "h%d" % (k - 1)], ["h%d" % k])
                if k == 1:
                    counting(T.n0[:], T.hist[:, HW + 1:HW + 1 + C], hv(1), ["h1"], "n0")
            elif w == "E" and k in PAR["ea"] + PAR["eb"]:
                op("s", lambda: s.activation(sl("sg", k), S, F.Sign, bias=hv(k + 1), scale=-1.0), ["S", "h%d" % (k + 1)], ["s%d" % k])
                if k in PAR["eb"]:
                    op("s", lambda: s.activation(sl("fl", k), sl("sg", k), F.Abs), ["s%d" % k], ["f%d" % k])
                continue
            elif w == "E":
                ts(sl("fl", k), S, hv(k + 1), None, A.is_equal, None, ["S", "h%d" % (k + 1)], ["f%d" % k])
            elif w == "H":
                if k not in PAR["ea"]:
                    continue
                ts(sl("fl", k), sl("sg", k), 0.0, None, A.is_equal, None, ["s%d" % k], ["f%d" % k])
            elif w == "Q":
                if k in PAR["eb"]:
                    op("v", lambda: v.tensor_tensor_scan(sl("cu", k), T.one[:], sl("fl", k), 0.5, A.add, A.subtract), ["f%d" % k, "one"], ["q%d" % k])
                else:
                    op("v", lambda: v.tensor_tensor_scan(sl("cu", k), sl("fl", k), sl("fl", k), 0.5, A.add, A.max), ["f%d" % k], ["q%d" % k])
                todo.append(k)
                flush()
            elif w == "O":
                a, b = (1, 4) if k == 1 else (4, 8)
                op("v", lambda: v.tensor_tensor(T.ep[:, a:b], T.hist[:, HW * (a + 1) + C:HW * (b + 1):HW], T.hist[:, HW * a + C:HW * b:HW], A.is_equal),
                   ["h%d" % i for i in range(a, b + 1)], ["ep%d" % k])
                if k == 1:
                    ts(T.cn[:, 0:1], T.n0[:], 2.0, -384.0, A.mult, A.add, ["n0"], ["c0"])
            else:
                a, b = (0, 4) if k == 1 else (4, 8)
                op("v", lambda: v.tensor_tensor_scan(T.ob[:, a:b], T.ep[:, a:b], T.ones[:, a:b], T.ob[:, 3:4] if a else 0.0, A.mult, A.add),
                   (["ob0", "ep2"] if a else ["ep0", "ep1"]) + ["ones"], ["ob%d" % (k - 1)])
                ready.update(range(a, b))
                flush()
            yield
        while late:
            move(late.pop())
        for _ in spread("n32", ["n32z"] + ["n32%d%d" % (G, a) for G in range(4) for a in range(4)], "nd", "no"):
            yield
        on = "on%d" % rd
        ts(T[on][:], T.no[:].indirect(T.ordn[:, 0:1]), 0.5, 192.0, A.mult, A.add, ["no", "ordn"], [on])
        yield

    for rd in (1, 2, 3):
        xq, xz, uq, uz = "xq%d" % (rd - 1), "xz%d" % (rd - 1), "uq%d" % (rd - 1), "uz%d" % (rd - 1)
        nq, nz, on = "xq%d" % rd, "xz%d" % rd, "on%d" % rd
        uk, xk, nk = ["U%d" % (rd - 1)], ["X%d%d" % (rd - 1, h) for h in (0, 1)], ["X%d%d" % (rd, h) for h in (0, 1)]

        def unpack(bank, h, b):
            mm(bank, "efq", "efz", 128 * b, xq, xz, HALF[h][0], HALF[h][1], [xk[h]], True, False)

        def ahead():
            for b in range(4):
                unpack(BANKS[0][b], 0, b)
            for b in range(2):
                unpack(BANKS[1][b], 1, b)
        if rd > 1:
            ahead()
        mm(SB, uq, uz, 0, xq, xz, 0, C, uk + xk, True, True)
        mm(S2, uq, uz, 0, xq, xz, 0, C, uk + xk, True, True)
        if rd == 1:
            ahead()
        fill = top8(rd)
        slots = iter(PAR["down"])

        def gap(n=None):
            n = next(slots, 0) if n is None else n
            for _ in range(n):
                next(fill, None)
        op("v", lambda: v.transpose(T.st[:], P[SB][:, 0:C]), ["p%d" % SB], ["st"])
        cp("s", T.ssb[:], P[S2][:, 0:C], ["p%d" % S2], ["S"])
        for b in (2, 3):
            unpack(BANKS[1][b], 1, b)
        gap()
        op("v", lambda: v.tensor_tensor_scan(T.ex[:, 1:C], T.st[:, 0:C - 1], T.cap[:, 1:C], -BIG, A.max, A.min), ["st", "cap"], ["ex"])
        gap()
        op("v", lambda: v.tensor_tensor(T.nr[:], T.st[:], T.ex[:], A.is_le), ["st", "ex", "ex0"], ["nr"])
        gap()
        if rd == 1:
            op("v", lambda: v.quantize_mx(T.eeq[:], T.eez[:], T.ee[:]), ["ee"], ["eeq"])
        op("v", lambda: v.tensor_tensor_scan(T.tr[:], T.nr[:], T.nr[:], 0.0, A.mult, A.add), ["nr"], ["tr"])
        gap()
        for i in range(2):
            ts(T.k32[:, 12 * i:12 * i + 12], T.tr[:, 15 + 16 * i:C:32], -1.0, T.pf[:, 2 + i:3 + i], A.mult, A.add, ["tr", "pf%d" % (2 + i)], ["k32%d" % i])
        gap()
        for _ in spread("k32", ["k320", "k321", "k32z"], "kd", "ko"):
            gap()
        if rd == 1:
            op("v", lambda: v.quantize_mx(T.eoq[:], T.eoz[:], T.eo[:]), ["eo%d" % b for b in range(4)], ["eoq"])
        op("v", lambda: v.tensor_copy(T.ok[:], T.ko[:].indirect(T.ordk[:, 0:3])), ["ko", "ordk"], ["ok"])
        gap()
        for h, (c, d) in enumerate(HALF):
            for i, e in enumerate("eo"):
                pick("a%sq%d" % (e, rd), "a%sz%d" % (e, rd), uq, uz, "ok", 24 * i + c // 16, 24 * i + d // 16, c, d, uk + ["ok"], "a%s%d" % (e, h))
                for b in range(4):
                    mm(BANKS[h][b], "e%sq" % e, "e%sz" % e, 128 * b, "a%sq%d" % (e, rd), "a%sz%d" % (e, rd), c, d, ["a%s%dq" % (e, h), "a%s%dz" % (e, h)], False, e == "o")
        for h, (c, d) in enumerate(HALF):
            def take(q, b):
                cp(q, T.zt[:, 4 * c + b:4 * d:4], P[BANKS[h][b]][:, 0:d - c], ["p%d" % BANKS[h][b]], ["zt%d%d" % (h, b)], 1.0 / 64)
            for b in range(4):
                if b not in PAR["zv"]:
                    take("s", b)
            gap(PAR["z"][h])
            for b in PAR["zv"]:
                take("v", b)
            for b in range(4):
                unpack(BANKS[h][b], h, b)
            quant("zq", "zz", "zt", c, d, ["zt%d%d" % (h, b) for b in range(4)], ["Z%d" % h])
            for b in range(4):
                mm(BANKS[h][b], "wq", "wz", 128 * b, "zq", "zz", c, d, ["Z%d" % h, "wq0", "wz0"], False, True)
        for h, (c, d) in enumerate(HALF):
            def give(q, b):
                cp(q, T.xt[:, 4 * c + b:4 * d:4], P[BANKS[h][b]][:, 0:d - c], ["p%d" % BANKS[h][b]], ["xt%d%d" % (h, b)], 1.0 / 32)
            for b in range(4):
                if b not in PAR["xv"]:
                    give("s", b)
            gap(PAR["x"][h])
            for b in PAR["xv"]:
                give("v", b)
            quant(nq, nz, "xt", c, d, ["xt%d%d" % (h, b) for b in range(4)], [nk[h]])
        gap(99)
        for i, e in enumerate("eo"):
            pick("v%sq%d" % (e, rd), "v%sz%d" % (e, rd), nq, nz, on, 8 * i, 8 * i + 8, 0, 128, nk + [on], "v" + e)
            for b in range(4):
                mm(BANKS[0][b], "e%sq" % e, "e%sz" % e, 128 * b, "v%sq%d" % (e, rd), "v%sz%d" % (e, rd), 0, 128, ["v%sq" % e, "v%sz" % e], e == "e", e == "o")
        for b in range(4):
            cp("vs"[b % 2], T.vt[:, b:512:4], P[BANKS[0][b]][:, 0:128], ["p%d" % BANKS[0][b]], ["vt%d" % b], 1.0 / 32)
        quant("sq%d" % rd, "sz%d" % rd, "vt", 0, 128, ["vt%d" % b for b in range(4)], ["out"])
        dst = T.cores[(rank + STEP[rd - 1]) % N]
        rid, pid, _ = topo.addr(dst)
        eng = topo.engines(core, dst)
        half = len(eng) // 2
        m1 = sum(1 << e for e in eng[:half])
        m2 = sum(1 << e for e in eng[half:])
        before("p", ["out"], [])
        g.remote_dma(T["uq%d" % rd][:].bitcast(dt.uint8), T["sq%d" % rd][:].bitcast(dt.uint8), T.sem["rc%d" % rd], T.sem["sent"], pid, rid, m1)
        g.remote_dma(T["uz%d" % rd][:], T["sz%d" % rd][:], T.sem["rc%d" % rd], T.sem["sent"], pid, rid, m2)
        count["sent"] = count.get("sent", 0) + len(eng)
        count["rc%d" % rd] = len(eng)
        lastw["U%d" % rd] = {"rc%d" % rd: len(eng)}

    op("v", lambda: v.quantize_mx(T.vq[:], T.vz[:], T.vin[:]), ["vin"], ["vq"])
    mm(S2, "vq", "vz", 0, "xq3", "xz3", 0, C, nk, True, True)
    cp("s", T.yt[:], P[S2][:, 0:C], ["p%d" % S2], ["yt"])
    ts(T.nop[:], T.nd[:, :, 0, :], 0.5, 192.0, A.mult, A.add, ["nd0"], ["nop"])
    dma("y", T.oc[:], T.xq3[:].bitcast(dt.uint8), nk, [], "outy")
    for k in range(4):
        dma("y", T.osc[4 * k:4 * k + 4, :], T.xz3[32 * k:32 * k + 4, :], nk, [], "outy")
    for a in range(4):
        dma("y", T.op[2 * a:2 * a + 2, 0:C], T.kd[32 * a:32 * a + 24, :, 0, :], ["kd0"], [], "outy")
    dma("s", T.y[:], T.yt[:], ["yt"], [], "outs")
    for a in range(4):
        for i in range(2):
            dma("y" if i else "s", T.op[2 * a + i, C:C + 128], T.nop[32 * a + i:32 * a + 8:2, :, :], ["nop"], [], "outy" if i else "outs")
    dma("s", T.uc[:], T.uq3[:].bitcast(dt.uint8), ["U3"], [], "outs")
    for k in range(4):
        dma("y" if k % 2 else "s", T.usc[4 * k:4 * k + 4, :], T.uz3[32 * k:32 * k + 4, :], ["U3"], [], "outy" if k % 2 else "outs")
    for sem in sorted(count):
        wait("p", (sem, count[sem]))
